import numpy as np
import ml_dtypes


def mxq(x, axis, fmt="e4m3"):
    dtype, down = {"e4m3": (ml_dtypes.float8_e4m3fn, 7), "e5m2": (ml_dtypes.float8_e5m2, 14)}[fmt]
    v = np.moveaxis(np.asarray(x, np.float32).astype(ml_dtypes.bfloat16).astype(np.float64), axis, -1)
    blocks = v.reshape(v.shape[:-1] + (-1, 32))
    amax = np.abs(blocks).max(-1, keepdims=True)
    byte = np.maximum(np.where(amax > 0, np.frexp(amax)[1] - 1 + 127, 0) - down, 1)
    scale = np.exp2(byte - 127.0)
    codes = (blocks / scale).astype(np.float32).astype(dtype).astype(np.float64)
    return np.moveaxis((codes * scale).reshape(v.shape), -1, axis)


WIDE = False


def mx_kscale(k):
    if not WIDE:
        return np.ones(k)
    levels = np.array([10, -10, 5, -5, 0])
    if k % 512:
        return np.exp2(np.random.permutation(np.resize(levels, k // 32))).repeat(32)
    a = np.empty((k // 512, 16))
    for p in range(k // 512):
        a[p, :8] = np.random.permutation(np.resize(levels, 8))
        for g in range(8):
            far = levels[np.abs(levels - a[p, g]) >= 10]
            a[p, g + 8] = far[np.random.randint(len(far))]
    return np.exp2(a.ravel()).repeat(32)


BF16 = ml_dtypes.bfloat16


def bf(x):
    return np.asarray(x, np.float32).astype(BF16)


def f64(x):
    return np.asarray(x).astype(np.float64)

def planes(Y):
    n, m = Y.shape
    b = f64(bf(Y)).reshape(n // 32, 32, m)
    amax = np.abs(b).max(1)
    byte = np.clip(np.where(amax > 0, np.frexp(amax)[1] - 1 + 127 - 7, 1), 1, 254)
    codes = (b * np.exp2(127.0 - byte)[:, None, :]).reshape(n, m).astype(np.float32).astype(ml_dtypes.float8_e4m3fn).view(np.uint8)
    words = codes.reshape(n // 512, 128, 4, m).transpose(0, 1, 3, 2)
    return np.ascontiguousarray(words), np.ascontiguousarray(byte.astype(np.uint8).reshape(n // 512, 16, m))


H, T, DK = 4, 1024, 512


def setup_inputs():
    s = mx_kscale(DK)
    queries = np.random.randn(H, T, DK)
    strength = np.exp(0.8 * np.random.randn(H, T, 1))
    keys = np.random.randn(H, T, DK) * strength / np.sqrt(DK)
    rate = np.linspace(1.0, 3.0, H)[:, None]
    clock = rate * np.cumsum(np.abs(np.random.randn(H, T)), axis=1) / T
    return {
        "queries": bf(queries * s),
        "keys": bf(keys / s),
        "clock": bf(clock),
    }


def reference(queries, keys, clock):
    qq = mxq(f64(queries), 2, "e4m3")
    kq = mxq(f64(keys), 2, "e4m3")
    b = f64(clock)
    raw = qq @ kq.swapaxes(1, 2)
    dist = np.abs(b[:, :, None] - b[:, None, :])
    y = raw / np.exp(dist)
    Y = y.reshape(H * T, T).T
    words, scales = planes(Y)
    return y, words, scales

@@ -1,0 +1,333 @@
+from contextlib import ExitStack
+
+import concourse.mybir as mybir
+from concourse.masks import make_identity
+
+H, T, DK = 4, 1024, 512
+FLOPS = 2 * H * T * T * DK
+
+F32 = mybir.dt.float32
+BF16 = mybir.dt.bfloat16
+I32 = mybir.dt.int32
+U32 = mybir.dt.uint32
+U8 = mybir.dt.uint8
+FP8X4 = mybir.dt.float8_e4m3fn_x4
+ALU = mybir.AluOpType
+ACT = mybir.ActivationFunctionType
+
+P = 128
+BLOCKS = T // P
+STEPS = H * BLOCKS
+UNIT = 256
+HALF = 512
+LEVELS = (512, 256, 128)
+START, END = 0, 1
+Y_BUFS = 10
+WARM = 16
+GROUPS = [[4, 4], [4, 4], [4, 4], [4, 2, 1, 1]]
+
+
+def far_segments(block):
+    found = []
+    for level, width in enumerate(LEVELS):
+        base = block * P // (2 * width) * (2 * width)
+        middle = base + width
+        if block * P < middle:
+            found.append((level, middle, width, START, middle // P))
+        else:
+            found.append((level, base, width, END, middle // P - 1))
+    return found
+
+
+def tile_bidirectional_decay_scores_g1_kernel(tc, queries, keys, clock, out_0, out_1, out_2):
+    nc = tc.nc
+    with ExitStack() as ctx:
+        sb = ctx.enter_context(tc.tile_pool(name="sb", bufs=1))
+        ps = ctx.enter_context(tc.psum_pool(name="ps", bufs=1))
+        ctx.enter_context(tc.manual_schedule())
+
+        counters = {}
+
+        def rotating(pool, tag, slots, shape, dtype, **extra):
+            n = counters.get(tag, 0)
+            counters[tag] = n + 1
+            return pool.tile(shape, dtype, name="%s_%d" % (tag, n), tag="%s%d" % (tag, n % slots), **extra)
+
+        source = {"q": queries, "k": keys}
+        raw_in = {}
+
+        def load(which, h, half, units):
+            if (which, h, half) not in raw_in:
+                raw_in[which, h, half] = sb.tile([P, 2, 2 * DK], BF16, name="in_%s%d%d" % (which, h, half), align_bytes=64)
+            rows = source[which][h, half * HALF : (half + 1) * HALF, :].rearrange("(b p j) c -> p b (j c)", b=2, j=2)
+            nc.sync.dma_start(out=raw_in[which, h, half][:, units, :], in_=rows[:, units, :])
+
+        clock_rows = sb.tile([P, P], BF16, name="clock_rows", align_bytes=64)
+        nc.vector.memset(clock_rows[:], 0.0)
+        load("k", 0, 0, slice(0, 1))
+        nc.sync.dma_start(out=clock_rows[0:STEPS, :], in_=clock.rearrange("h (b p) -> (h b) p", p=P))
+        load("k", 0, 0, slice(1, 2))
+        load("q", 0, 0, slice(0, 1))
+        load("k", 0, 1, slice(0, 1))
+        load("k", 0, 1, slice(1, 2))
+        load("q", 0, 0, slice(1, 2))
+        load("q", 0, 1, slice(0, 2))
+        for h in range(1, H):
+            for which, half in (("k", 0), ("k", 1), ("q", 0), ("q", 1)):
+                load(which, h, half, slice(0, 2))
+
+        table_warm = sb.tile([P, 1], F32, name="table_warm")
+        ones = sb.tile([P, 4 * P], BF16, name="ones", align_bytes=64)
+        nc.vector.memset(ones[:].bitcast(F32), 1.0)
+        nc.scalar.activation(out=table_warm[:], in_=ones[:, 0:1], func=ACT.Exp)
+        ident_bf = sb.tile([P, P], BF16, name="ident_bf", align_bytes=64)
+        ident_f32 = sb.tile([P, P], F32, name="ident_f32", align_bytes=64)
+        make_identity(nc, ident_bf[:])
+        make_identity(nc, ident_f32[:])
+        warm_codes = sb.tile([P, P], U32, name="warm_codes", align_bytes=64)
+        warm_scales = sb.tile([P, P], U8, name="warm_scales", align_bytes=64)
+        nc.vector.quantize_mx(out=warm_codes[:].bitcast(FP8X4), scales=warm_scales[:], in_=ones[:])
+
+        def warm(count):
+            bank = rotating(ps, "raw", 4, [P, HALF], F32)
+            for n in range(count):
+                nc.tensor.matmul_mx(out=bank[:, n % 4 * P : (n % 4 + 1) * P], lhsT=warm_codes[:].bitcast(FP8X4), lhsT_scale=warm_scales[:],
+                                    rhs=warm_codes[:].bitcast(FP8X4), rhs_scale=warm_scales[:], start=True, stop=True)
+
+        warm(WARM)
+
+        bank = rotating(ps, "turn_out", 2, [P, 3, P], BF16)
+        nc.tensor.transpose(bank[:, 0, :], clock_rows[:], ident_bf[:])
+        nc.tensor.transpose(bank[:, 1, :], clock_rows[:, 0:1].to_broadcast([P, P]), ident_bf[:])
+        nc.tensor.transpose(bank[:, 2, :], clock_rows[:, P - 1 : P].to_broadcast([P, P]), ident_bf[:])
+        col_bf = sb.tile([P, STEPS], BF16, name="col_bf")
+        col = sb.tile([P, STEPS], F32, name="col")
+        refs = sb.tile([P, H, 2, BLOCKS], F32, name="refs")
+        neg_end = sb.tile([P, STEPS], F32, name="neg_end")
+        nc.vector.tensor_copy(out=col_bf[:], in_=bank[:, 0, 0:STEPS])
+        nc.vector.tensor_copy(out=col[:], in_=bank[:, 0, 0:STEPS])
+        nc.vector.tensor_copy(out=refs[:], in_=bank[:, 1:3, 0:STEPS].rearrange("p e (h j) -> p h e j", h=H))
+        nc.vector.tensor_scalar(out=neg_end[:], in0=bank[:, 2, 0:STEPS], scalar1=-1.0, scalar2=None, op0=ALU.mult)
+        gaps = sb.tile([P, H, BLOCKS, 2 * BLOCKS], F32, name="gaps")
+        gaps_abs = sb.tile([P, H, BLOCKS * 2 * BLOCKS], F32, name="gaps_abs")
+        near = sb.tile([P, H, BLOCKS * 2 * BLOCKS], F32, name="near")
+        for h in range(H):
+            nc.vector.tensor_tensor(
+                out=gaps[:, h, :, :],
+                in0=col[:, h * BLOCKS : (h + 1) * BLOCKS].unsqueeze(2).to_broadcast([P, BLOCKS, 2 * BLOCKS]),
+                in1=refs[:, h, :, :].rearrange("p e j -> p (e j)").unsqueeze(1).to_broadcast([P, BLOCKS, 2 * BLOCKS]),
+                op=ALU.subtract)
+
+        clock_wide = {}
+
+        wide_banks = {}
+
+        def spread_clock(h):
+            wide_bank = rotating(ps, "turn_out", 2, [P, T], BF16)
+            wide_banks[h] = wide_bank
+            for b in range(BLOCKS):
+                n = h * BLOCKS + b
+                nc.tensor.transpose(wide_bank[:, b * P : (b + 1) * P], col_bf[:, n : n + 1].to_broadcast([P, P]), ident_bf[:])
+
+        def keep_clock(h, engine_copy):
+            clock_wide[h] = rotating(sb, "clock_wide", 2, [P, T], BF16, align_bytes=64)
+            engine_copy(out=clock_wide[h][:], in_=wide_banks[h][:])
+
+        far_rows, diag = {}, {}
+
+        def head_job(h):
+            far_rows[h] = rotating(sb, "far_rows", 2, [P, len(LEVELS), T], F32, align_bytes=64)
+            diag[h] = rotating(sb, "diag", 2, [P, T], F32, align_bytes=64)
+            nc.scalar.activation(out=gaps_abs[:, h, :], in_=gaps[:, h, :, :].rearrange("p i r -> p (i r)"), func=ACT.Abs)
+            nc.scalar.activation(out=near[:, h, :], in_=gaps_abs[:, h, :], func=ACT.Exp, scale=-1.0)
+
+        made = set()
+
+        def block_job(s):
+            h, block = divmod(s, BLOCKS)
+            cols = slice(block * P, (block + 1) * P)
+            dist = rotating(sb, "dist", 2, [P, P], F32, align_bytes=64)
+            nc.scalar.activation(out=dist[:], in_=clock_wide[h][:, cols], func=ACT.Abs, scale=-1.0, bias=col[:, s : s + 1])
+            if block == 0:
+                head_job(h)
+            for level, first, width, side, ref_block in far_segments(block):
+                if (h, level, first) in made:
+                    continue
+                made.add((h, level, first))
+                seg = slice(first, first + width)
+                if side == START:
+                    nc.scalar.activation(out=far_rows[h][:, level, seg], in_=clock_wide[h][:, seg], func=ACT.Exp,
+                                         scale=-1.0, bias=refs[:, h, START, ref_block : ref_block + 1])
+                else:
+                    n = h * BLOCKS + ref_block
+                    nc.scalar.activation(out=far_rows[h][:, level, seg], in_=clock_wide[h][:, seg], func=ACT.Exp,
+                                         scale=1.0, bias=neg_end[:, n : n + 1])
+            nc.scalar.activation(out=diag[h][:, cols], in_=dist[:], func=ACT.Exp, scale=-1.0)
+
+        grouped_in, codes, scales = {}, {}, {}
+
+        def turn_in(which, h, half, b, engine_copy):
+            words = raw_in[which, h, half][:, b, :].bitcast(F32)
+            turned = rotating(ps, "turn_in", 2, [P, 4, P], F32)
+            for j in range(2):
+                for u in range(2):
+                    nc.tensor.transpose(turned[:, 2 * j + u, :], words[:, 256 * j + u : 256 * (j + 1) : 2], ident_f32[:])
+            if b == 0:
+                grouped_in[which, h, half] = rotating(sb, "grouped_in", 3, [P, 4 * HALF], BF16, align_bytes=64)
+            target = grouped_in[which, h, half][:, b * 4 * UNIT : (b + 1) * 4 * UNIT].bitcast(F32)
+            engine_copy(out=target.rearrange("k (p a) -> k p a", a=4), in_=turned[:].rearrange("k a p -> k p a"))
+
+        def quantize_in(which, h, half, first, count):
+            if first == 0:
+                codes[which, h, half] = rotating(sb, "codes_" + which, 4, [P, HALF], U32, align_bytes=64)
+                scales[which, h, half] = rotating(sb, "scales_" + which, 4, [P, HALF], U8, align_bytes=64)
+            rows = slice(first * UNIT, (first + count) * UNIT)
+            nc.vector.quantize_mx(out=codes[which, h, half][:, rows].bitcast(FP8X4), scales=scales[which, h, half][:, rows],
+                                  in_=grouped_in[which, h, half][:, 4 * first * UNIT : 4 * (first + count) * UNIT])
+
+        raw = {}
+
+        def multiply(s, g):
+            h, block = divmod(s, BLOCKS)
+            half, place = divmod(block, 4)
+            cols = slice(place * P, (place + 1) * P)
+            raw[s, g] = rotating(ps, "raw", 4, [P, HALF], F32)
+            nc.tensor.matmul_mx(out=raw[s, g][:], lhsT=codes["q", h, half][:, cols].bitcast(FP8X4), lhsT_scale=scales["q", h, half][:, cols],
+                                rhs=codes["k", h, g][:].bitcast(FP8X4), rhs_scale=scales["k", h, g][:], start=True, stop=True)
+
+        y = {}
+
+        def weigh(s):
+            h, block = divmod(s, BLOCKS)
+            y[s] = rotating(sb, "y", Y_BUFS, [P, T], F32, align_bytes=64)
+            parts = [(first, width, level, side, ref_block) for level, first, width, side, ref_block in far_segments(block)]
+            parts.append((block * P, P, None, None, None))
+            for first, width, level, side, ref_block in sorted(parts, key=lambda part: part[0]):
+                g, local = divmod(first, HALF)
+                seg = slice(first, first + width)
+                scores = raw[s, g][:, local : local + width]
+                if level is None:
+                    nc.vector.tensor_tensor(out=y[s][:, seg], in0=scores, in1=diag[h][:, seg], op=ALU.mult)
+                else:
+                    n = (block * 2 + side) * BLOCKS + ref_block
+                    nc.vector.scalar_tensor_tensor(out=y[s][:, seg], in0=scores, scalar=near[:, h, n : n + 1],
+                                                   in1=far_rows[h][:, level, seg], op0=ALU.mult, op1=ALU.mult)
+            nc.sync.dma_start(out=out_0[h, block * P : (block + 1) * P, :], in_=y[s][:])
+
+        rounded = {}
+
+        def round_y(s):
+            rounded[s] = rotating(sb, "rounded", 3, [P, T], BF16, align_bytes=64)
+            target = rounded[s][:].rearrange("i (u a e) -> i u a e", u=2, e=2)
+            values = y[s][:].rearrange("i (a u e) -> i u a e", u=2, e=2)
+            if s < STEPS - 1:
+                nc.gpsimd.tensor_scalar(out=target, in0=values, scalar1=1.0, scalar2=1.0, op0=ALU.mult, op1=ALU.mult)
+            else:
+                nc.vector.tensor_copy(out=target, in_=values)
+
+        group_of = {}
+        for h in range(H):
+            first = h * BLOCKS
+            for size in GROUPS[h]:
+                for s in range(first, first + size):
+                    group_of[s] = (first, size)
+                first += size
+        grouped_out, out_words, out_scales = {}, {}, {}
+
+        def turn_out(s):
+            first, size = group_of[s]
+            words = rounded[s][:].bitcast(F32)
+            turned = rotating(ps, "turn_out", 2, [P, 2, 2, P], F32)
+            for g in range(2):
+                for u in range(2):
+                    at = 256 * u + P * g
+                    nc.tensor.transpose(turned[:, g, u, :], words[:, at : at + P], ident_f32[:])
+            if s == first:
+                grouped_out[first] = rotating(sb, "grouped_out", 2, [P, 2, 4 * size * P], BF16, align_bytes=64)
+            place = s - first
+            target = grouped_out[first][:, :, 4 * place * P : 4 * (place + 1) * P].bitcast(F32)
+            nc.scalar.copy(out=target.rearrange("k g (r u) -> k g r u", u=2), in_=turned[:].rearrange("k g u r -> k g r u"))
+
+        words_hbm = out_1.rearrange("g p m t -> p g (m t)")
+
+        def quantize_out(first, g):
+            size = group_of[first][1]
+            h, block = divmod(first, BLOCKS)
+            if g == 0:
+                out_words[first] = rotating(sb, "out_words", 3, [P, 2, size * P], U32, align_bytes=64)
+                if block == 0:
+                    out_scales[h] = sb.tile([P, 2, T], U8, name="out_scales%d" % h, align_bytes=64)
+            nc.vector.quantize_mx(out=out_words[first][:, g, :].bitcast(FP8X4),
+                                  scales=out_scales[h][:, g, block * P : (block + size) * P], in_=grouped_out[first][:, g, :])
+            if g == 1:
+                nc.sync.dma_start(out=words_hbm[:, :, 4 * first * P : 4 * (first + size) * P].bitcast(I32),
+                                  in_=out_words[first][:].bitcast(I32))
+                if block + size == BLOCKS:
+                    for quad in range(4):
+                        nc.sync.dma_start(
+                            out=out_2[:, 4 * quad : 4 * quad + 4, h * T : (h + 1) * T].rearrange("g r m -> r g m").bitcast(I32),
+                            in_=out_scales[h][32 * quad : 32 * quad + 4, :, :].bitcast(I32))
+
+        vcopy, scopy = nc.vector.tensor_copy, nc.scalar.copy
+        turn_in("k", 0, 0, 0, vcopy)
+        spread_clock(0)
+        keep_clock(0, scopy)
+        turn_in("k", 0, 0, 1, vcopy)
+        block_job(0)
+        turn_in("q", 0, 0, 0, vcopy)
+        quantize_in("k", 0, 0, 0, 2)
+        turn_in("k", 0, 1, 0, vcopy)
+        quantize_in("q", 0, 0, 0, 1)
+        multiply(0, 0)
+        turn_in("k", 0, 1, 1, scopy)
+        block_job(1)
+        turn_in("q", 0, 0, 1, vcopy)
+        quantize_in("k", 0, 1, 0, 2)
+        multiply(0, 1)
+        quantize_in("q", 0, 0, 1, 1)
+
+        units = [("q", 0, 1, 0), ("q", 0, 1, 1)]
+        for h in range(1, H):
+            for which, half in (("k", 0), ("k", 1), ("q", 0), ("q", 1)):
+                units.extend([(which, h, half, 0), (which, h, half, 1)])
+        units_at = {0: units[0:2], 1: units[2:4]}
+        for n in range(4, len(units)):
+            units_at[n - 2] = [units[n]]
+        quant_at = {}
+        for s, listed in units_at.items():
+            if listed[-1][3] == 1:
+                quant_at[s + 1] = [("in",) + listed[-1][0:3]]
+        for first in range(0, 24, 4):
+            quant_at[first + 7] = [("out", first, 0)]
+            quant_at[first + 9] = [("out", first, 1)]
+        quant_at[30] = [("out", 24, 0)]
+        quant_at[31] = [("out", 24, 1)]
+        quant_at[32] = [("out", 28, 0), ("out", 28, 1)]
+        quant_at[33] = [("out", 30, 0), ("out", 30, 1)]
+        quant_at[34] = [("out", 31, 0), ("out", 31, 1)]
+
+        for s in range(STEPS + 3):
+            if s + 1 < STEPS:
+                multiply(s + 1, 0)
+                multiply(s + 1, 1)
+            if s + 2 < STEPS:
+                block_job(s + 2)
+            for which, h, half, b in units_at.get(s, []):
+                turn_in(which, h, half, b, scopy)
+            if 2 <= s < STEPS + 2:
+                turn_out(s - 2)
+            if s < STEPS:
+                weigh(s)
+            if s % BLOCKS == 3 and s + BLOCKS < STEPS:
+                spread_clock(s // BLOCKS + 1)
+            if s % BLOCKS == 4 and s + BLOCKS < STEPS:
+                keep_clock(s // BLOCKS + 1, vcopy)
+            if s < STEPS - 1:
+                round_y(s)
+            for job in quant_at.get(s, []):
+                if job[0] == "in":
+                    quantize_in(job[1], job[2], job[3], 0, 2)
+                else:
+                    quantize_out(job[1], job[2])
+            if s == STEPS - 1:
+                round_y(s)

@@ -20,22 +20,19 @@ BLOCKS = T // P
 STEPS = H * BLOCKS
 UNIT = 256
 HALF = 512
-LEVELS = (512, 256, 128)
 START, END = 0, 1
 Y_BUFS = 10
-WARM = 16
-GROUPS = [[4, 4], [4, 4], [4, 4], [4, 2, 1, 1]]
+WARM = 12
+GROUPS = [[4, 4], [4, 4], [4, 4], [2, 2, 2, 2]]
+ROWS = 2
 
 
 def far_segments(block):
     found = []
-    for level, width in enumerate(LEVELS):
-        base = block * P // (2 * width) * (2 * width)
-        middle = base + width
-        if block * P < middle:
-            found.append((level, middle, width, START, middle // P))
-        else:
-            found.append((level, base, width, END, middle // P - 1))
+    for other in range(BLOCKS):
+        if other != block:
+            side = START if other > block else END
+            found.append((side, other * P, P, side, other))
     return found
 
 
@@ -48,139 +45,191 @@ def tile_bidirectional_decay_scores_g1_kernel(tc, queries, keys, clock, out_0, o
 
         counters = {}
 
-        def rotating(pool, tag, slots, shape, dtype, **extra):
+        def slot(tag, slots):
             n = counters.get(tag, 0)
             counters[tag] = n + 1
-            return pool.tile(shape, dtype, name="%s_%d" % (tag, n), tag="%s%d" % (tag, n % slots), **extra)
+            return dict(name="%s_%d" % (tag, n), tag="%s%d" % (tag, n % slots))
+
+        def sbuf(tag, slots, shape, dtype):
+            return sb.tile(shape, dtype, align_bytes=64, **slot(tag, slots))
+
+        def psum(tag, slots, shape, dtype):
+            return ps.tile(shape, dtype, **slot(tag, slots))
+
+        vcopy, scopy = nc.vector.tensor_copy, nc.scalar.copy
 
         source = {"q": queries, "k": keys}
         raw_in = {}
 
-        def load(which, h, half, units):
-            if (which, h, half) not in raw_in:
-                raw_in[which, h, half] = sb.tile([P, 2, 2 * DK], BF16, name="in_%s%d%d" % (which, h, half), align_bytes=64)
-            rows = source[which][h, half * HALF : (half + 1) * HALF, :].rearrange("(b p j) c -> p b (j c)", b=2, j=2)
-            nc.sync.dma_start(out=raw_in[which, h, half][:, units, :], in_=rows[:, units, :])
+        def load_unit(which, h, half, b):
+            if b == 0:
+                raw_in[which, h, half] = sbuf("raw_in", 4 * H, [P, 2, 2 * DK], BF16)
+            first = half * HALF + b * UNIT
+            nc.sync.dma_start(out=raw_in[which, h, half][:, b, :],
+                              in_=source[which][h, first : first + UNIT, :].rearrange("(p j) c -> p (j c)", j=2))
 
-        clock_rows = sb.tile([P, P], BF16, name="clock_rows", align_bytes=64)
-        nc.vector.memset(clock_rows[:], 0.0)
-        load("k", 0, 0, slice(0, 1))
+        def load_half(which, h, half):
+            raw_in[which, h, half] = sbuf("raw_in", 4 * H, [P, 2, 2 * DK], BF16)
+            nc.sync.dma_start(out=raw_in[which, h, half][:].rearrange("p b x -> p (b x)"),
+                              in_=source[which][h, half * HALF : (half + 1) * HALF, :].rearrange("(p j) c -> p (j c)", j=4))
+
+        clock_rows = sbuf("clock_rows", 1, [P, P], BF16)
         nc.sync.dma_start(out=clock_rows[0:STEPS, :], in_=clock.rearrange("h (b p) -> (h b) p", p=P))
-        load("k", 0, 0, slice(1, 2))
-        load("q", 0, 0, slice(0, 1))
-        load("k", 0, 1, slice(0, 1))
-        load("k", 0, 1, slice(1, 2))
-        load("q", 0, 0, slice(1, 2))
-        load("q", 0, 1, slice(0, 2))
+        by_units = [("k", 0, 0), ("q", 0, 0), ("k", 0, 1)]
+        for which, h, half, b in (("k", 0, 0, 0), ("k", 0, 0, 1), ("q", 0, 0, 0), ("k", 0, 1, 0), ("k", 0, 1, 1), ("q", 0, 0, 1)):
+            load_unit(which, h, half, b)
+        load_half("q", 0, 1)
+        later_clocks = sbuf("later_clocks", 1, [P, (H - 1) * T], BF16)
         for h in range(1, H):
             for which, half in (("k", 0), ("k", 1), ("q", 0), ("q", 1)):
-                load(which, h, half, slice(0, 2))
+                load_half(which, h, half)
+                if (h, which, half) == (1, "k", 1):
+                    nc.sync.dma_start(out=later_clocks[:], in_=clock[1:H, :].rearrange("h t -> (h t)").partition_broadcast(P))
 
-        table_warm = sb.tile([P, 1], F32, name="table_warm")
-        ones = sb.tile([P, 4 * P], BF16, name="ones", align_bytes=64)
+        table_warm = sbuf("table_warm", 1, [P, 1], F32)
+        ones = sbuf("ones", 1, [P, 4 * P], BF16)
         nc.vector.memset(ones[:].bitcast(F32), 1.0)
         nc.scalar.activation(out=table_warm[:], in_=ones[:, 0:1], func=ACT.Exp)
-        ident_bf = sb.tile([P, P], BF16, name="ident_bf", align_bytes=64)
-        ident_f32 = sb.tile([P, P], F32, name="ident_f32", align_bytes=64)
+        ident_bf = sbuf("ident_bf", 1, [P, P], BF16)
+        ident_f32 = sbuf("ident_f32", 1, [P, P], F32)
         make_identity(nc, ident_bf[:])
         make_identity(nc, ident_f32[:])
-        warm_codes = sb.tile([P, P], U32, name="warm_codes", align_bytes=64)
-        warm_scales = sb.tile([P, P], U8, name="warm_scales", align_bytes=64)
+        warm_codes = sbuf("warm_codes", 1, [P, P], U32)
+        warm_scales = sbuf("warm_scales", 1, [P, P], U8)
         nc.vector.quantize_mx(out=warm_codes[:].bitcast(FP8X4), scales=warm_scales[:], in_=ones[:])
+        nc.vector.memset(clock_rows[32:64, :], 0.0)
+        nc.vector.memset(clock_rows[64:P, :], 0.0)
 
         def warm(count):
-            bank = rotating(ps, "raw", 4, [P, HALF], F32)
+            bank = ps.tile([P, HALF], F32, name="warm_bank", tag="raw00")
             for n in range(count):
                 nc.tensor.matmul_mx(out=bank[:, n % 4 * P : (n % 4 + 1) * P], lhsT=warm_codes[:].bitcast(FP8X4), lhsT_scale=warm_scales[:],
                                     rhs=warm_codes[:].bitcast(FP8X4), rhs_scale=warm_scales[:], start=True, stop=True)
 
         warm(WARM)
 
-        bank = rotating(ps, "turn_out", 2, [P, 3, P], BF16)
+        bank = psum("turn_out", 2, [P, 3, P], BF16)
         nc.tensor.transpose(bank[:, 0, :], clock_rows[:], ident_bf[:])
         nc.tensor.transpose(bank[:, 1, :], clock_rows[:, 0:1].to_broadcast([P, P]), ident_bf[:])
         nc.tensor.transpose(bank[:, 2, :], clock_rows[:, P - 1 : P].to_broadcast([P, P]), ident_bf[:])
-        col_bf = sb.tile([P, STEPS], BF16, name="col_bf")
-        col = sb.tile([P, STEPS], F32, name="col")
-        refs = sb.tile([P, H, 2, BLOCKS], F32, name="refs")
-        neg_end = sb.tile([P, STEPS], F32, name="neg_end")
-        nc.vector.tensor_copy(out=col_bf[:], in_=bank[:, 0, 0:STEPS])
-        nc.vector.tensor_copy(out=col[:], in_=bank[:, 0, 0:STEPS])
-        nc.vector.tensor_copy(out=refs[:], in_=bank[:, 1:3, 0:STEPS].rearrange("p e (h j) -> p h e j", h=H))
-        nc.vector.tensor_scalar(out=neg_end[:], in0=bank[:, 2, 0:STEPS], scalar1=-1.0, scalar2=None, op0=ALU.mult)
-        gaps = sb.tile([P, H, BLOCKS, 2 * BLOCKS], F32, name="gaps")
-        gaps_abs = sb.tile([P, H, BLOCKS * 2 * BLOCKS], F32, name="gaps_abs")
-        near = sb.tile([P, H, BLOCKS * 2 * BLOCKS], F32, name="near")
+        marks = sbuf("marks", 1, [P, 3, STEPS], BF16)
+        vcopy(out=marks[:], in_=bank[:, :, 0:STEPS])
+        neg_end = sbuf("neg_end", 1, [P, STEPS], F32)
+        nc.gpsimd.tensor_scalar(out=neg_end[:], in0=marks[:, 2, :], scalar1=-1.0, scalar2=1.0, op0=ALU.mult, op1=ALU.mult)
+        gaps = sbuf("gaps", 1, [P, H, BLOCKS, 2, BLOCKS], F32)
+        near = sbuf("near", 1, [P, H, BLOCKS * 2 * BLOCKS], F32)
         for h in range(H):
-            nc.vector.tensor_tensor(
-                out=gaps[:, h, :, :],
-                in0=col[:, h * BLOCKS : (h + 1) * BLOCKS].unsqueeze(2).to_broadcast([P, BLOCKS, 2 * BLOCKS]),
-                in1=refs[:, h, :, :].rearrange("p e j -> p (e j)").unsqueeze(1).to_broadcast([P, BLOCKS, 2 * BLOCKS]),
+            blocks = slice(h * BLOCKS, (h + 1) * BLOCKS)
+            nc.gpsimd.tensor_tensor(
+                out=gaps[:, h, :, :, :],
+                in0=marks[:, 0, blocks].unsqueeze(2).unsqueeze(3).to_broadcast([P, BLOCKS, 2, BLOCKS]),
+                in1=marks[:, 1:3, blocks].unsqueeze(1).to_broadcast([P, BLOCKS, 2, BLOCKS]),
                 op=ALU.subtract)
 
-        clock_wide = {}
-
-        wide_banks = {}
+        clock_wide, wide_banks = {}, {}
+        for h in range(1, H):
+            clock_wide[h] = later_clocks[:, (h - 1) * T : h * T]
 
         def spread_clock(h):
-            wide_bank = rotating(ps, "turn_out", 2, [P, T], BF16)
-            wide_banks[h] = wide_bank
+            wide_banks[h] = psum("turn_out", 2, [P, T], BF16)
             for b in range(BLOCKS):
                 n = h * BLOCKS + b
-                nc.tensor.transpose(wide_bank[:, b * P : (b + 1) * P], col_bf[:, n : n + 1].to_broadcast([P, P]), ident_bf[:])
+                nc.tensor.transpose(wide_banks[h][:, b * P : (b + 1) * P], marks[:, 0, n : n + 1].to_broadcast([P, P]), ident_bf[:])
 
         def keep_clock(h, engine_copy):
-            clock_wide[h] = rotating(sb, "clock_wide", 2, [P, T], BF16, align_bytes=64)
+            clock_wide[h] = sbuf("clock_wide", 1, [P, T], BF16)[:]
             engine_copy(out=clock_wide[h][:], in_=wide_banks[h][:])
 
-        far_rows, diag = {}, {}
+        far_rows, diag, dist, gaps_abs = {}, {}, {}, {}
 
-        def head_job(h):
-            far_rows[h] = rotating(sb, "far_rows", 2, [P, len(LEVELS), T], F32, align_bytes=64)
-            diag[h] = rotating(sb, "diag", 2, [P, T], F32, align_bytes=64)
-            nc.scalar.activation(out=gaps_abs[:, h, :], in_=gaps[:, h, :, :].rearrange("p i r -> p (i r)"), func=ACT.Abs)
-            nc.scalar.activation(out=near[:, h, :], in_=gaps_abs[:, h, :], func=ACT.Exp, scale=-1.0)
+        def job_open_head(h):
+            far_rows[h] = sbuf("far_rows", 2, [P, ROWS, T], F32)
+            diag[h] = sbuf("diag", 2, [P, T], F32)
+            gaps_abs[h] = sbuf("gaps_abs", 2, [P, BLOCKS * 2 * BLOCKS], F32)
+            nc.scalar.activation(out=gaps_abs[h][:], in_=gaps[:, h, :, :, :].rearrange("p i e j -> p (i e j)"), func=ACT.Abs)
 
-        made = set()
+        def job_near(h):
+            nc.scalar.activation(out=near[:, h, :], in_=gaps_abs[h][:], func=ACT.Exp, scale=-1.0)
 
-        def block_job(s):
+        def job_dist(s):
             h, block = divmod(s, BLOCKS)
-            cols = slice(block * P, (block + 1) * P)
-            dist = rotating(sb, "dist", 2, [P, P], F32, align_bytes=64)
-            nc.scalar.activation(out=dist[:], in_=clock_wide[h][:, cols], func=ACT.Abs, scale=-1.0, bias=col[:, s : s + 1])
+            dist[s] = sbuf("dist", 3, [P, P], F32)
+            nc.scalar.activation(out=dist[s][:], in_=clock_wide[h][:, block * P : (block + 1) * P], func=ACT.Abs,
+                                 scale=-1.0, bias=marks[:, 0, s : s + 1])
+
+        def job_diag(s):
+            h, block = divmod(s, BLOCKS)
+            nc.scalar.activation(out=diag[h][:, block * P : (block + 1) * P], in_=dist[s][:], func=ACT.Exp, scale=-1.0)
+
+        def job_row(h, row, first, width, side, ref_block):
+            seg = slice(first, first + width)
+            n = h * BLOCKS + ref_block
+            if side == START:
+                nc.scalar.activation(out=far_rows[h][:, row, seg], in_=clock_wide[h][:, seg], func=ACT.Exp,
+                                     scale=-1.0, bias=marks[:, 1, n : n + 1])
+            else:
+                nc.scalar.activation(out=far_rows[h][:, row, seg], in_=clock_wide[h][:, seg], func=ACT.Exp,
+                                     scale=1.0, bias=neg_end[:, n : n + 1])
+
+        jobs = [(0, P, job_open_head, (0,)), (0, P, job_dist, (0,))]
+        made = set()
+        for s in range(STEPS):
+            h, block = divmod(s, BLOCKS)
             if block == 0:
-                head_job(h)
-            for level, first, width, side, ref_block in far_segments(block):
-                if (h, level, first) in made:
-                    continue
-                made.add((h, level, first))
-                seg = slice(first, first + width)
-                if side == START:
-                    nc.scalar.activation(out=far_rows[h][:, level, seg], in_=clock_wide[h][:, seg], func=ACT.Exp,
-                                         scale=-1.0, bias=refs[:, h, START, ref_block : ref_block + 1])
-                else:
-                    n = h * BLOCKS + ref_block
-                    nc.scalar.activation(out=far_rows[h][:, level, seg], in_=clock_wide[h][:, seg], func=ACT.Exp,
-                                         scale=1.0, bias=neg_end[:, n : n + 1])
-            nc.scalar.activation(out=diag[h][:, cols], in_=dist[:], func=ACT.Exp, scale=-1.0)
+                jobs.append((s, P, job_near, (h,)))
+            fresh = []
+            for seg in sorted(far_segments(block), key=lambda part: part[1]):
+                if (h, seg[0], seg[1]) not in made:
+                    made.add((h, seg[0], seg[1]))
+                    fresh.append((s, seg[2], job_row, (h,) + seg))
+            jobs.extend(fresh[:1])
+            jobs.append((s, P, job_diag, (s,)))
+            jobs.extend(fresh[1:])
+            if s + 1 < STEPS:
+                if block == BLOCKS - 1:
+                    jobs.append((s, P, job_open_head, (h + 1,)))
+                jobs.append((s, P, job_dist, (s + 1,)))
+        per_step = sum(job[1] for job in jobs) // STEPS
+        done = [0, 0]
+
+        def run_jobs(needed, target, head_limit):
+            while done[0] < len(jobs):
+                s, width, fn, args = jobs[done[0]]
+                if s > needed and (done[1] + width > target or s // BLOCKS > head_limit):
+                    break
+                fn(*args)
+                done[0] += 1
+                done[1] += width
 
         grouped_in, codes, scales = {}, {}, {}
 
-        def turn_in(which, h, half, b, engine_copy):
+        turned_in = {}
+
+        def turn_in(which, h, half, b, tag=None):
             words = raw_in[which, h, half][:, b, :].bitcast(F32)
-            turned = rotating(ps, "turn_in", 2, [P, 4, P], F32)
+            if tag is None:
+                turned_in[which, h, half, b] = psum("turn_in", 2, [P, 4, P], F32)
+            else:
+                turned_in[which, h, half, b] = ps.tile([P, 4, P], F32, name="early_" + tag, tag=tag)
             for j in range(2):
                 for u in range(2):
-                    nc.tensor.transpose(turned[:, 2 * j + u, :], words[:, 256 * j + u : 256 * (j + 1) : 2], ident_f32[:])
+                    nc.tensor.transpose(turned_in[which, h, half, b][:, 2 * j + u, :],
+                                        words[:, 256 * j + u : 256 * (j + 1) : 2], ident_f32[:])
+
+        def copy_in(which, h, half, b, engine_copy):
             if b == 0:
-                grouped_in[which, h, half] = rotating(sb, "grouped_in", 3, [P, 4 * HALF], BF16, align_bytes=64)
-            target = grouped_in[which, h, half][:, b * 4 * UNIT : (b + 1) * 4 * UNIT].bitcast(F32)
-            engine_copy(out=target.rearrange("k (p a) -> k p a", a=4), in_=turned[:].rearrange("k a p -> k p a"))
+                grouped_in[which, h, half] = sbuf("grouped_in", 4, [P, 4 * HALF], BF16)
+            words = grouped_in[which, h, half][:].bitcast(F32)
+            if (which, h, half) in by_units:
+                target = words.rearrange("k (b p a) -> k b p a", b=2, a=4)[:, b, :, :]
+            else:
+                target = words.rearrange("k (p b a) -> k b p a", b=2, a=4)[:, b, :, :]
+            engine_copy(out=target, in_=turned_in[which, h, half, b][:].rearrange("k a p -> k p a"))
 
         def quantize_in(which, h, half, first, count):
             if first == 0:
-                codes[which, h, half] = rotating(sb, "codes_" + which, 4, [P, HALF], U32, align_bytes=64)
-                scales[which, h, half] = rotating(sb, "scales_" + which, 4, [P, HALF], U8, align_bytes=64)
+                codes[which, h, half] = sbuf("codes_" + which, 4, [P, HALF], U32)
+                scales[which, h, half] = sbuf("scales_" + which, 4, [P, HALF], U8)
             rows = slice(first * UNIT, (first + count) * UNIT)
             nc.vector.quantize_mx(out=codes[which, h, half][:, rows].bitcast(FP8X4), scales=scales[which, h, half][:, rows],
                                   in_=grouped_in[which, h, half][:, 4 * first * UNIT : 4 * (first + count) * UNIT])
@@ -191,39 +240,46 @@ def tile_bidirectional_decay_scores_g1_kernel(tc, queries, keys, clock, out_0, o
             h, block = divmod(s, BLOCKS)
             half, place = divmod(block, 4)
             cols = slice(place * P, (place + 1) * P)
-            raw[s, g] = rotating(ps, "raw", 4, [P, HALF], F32)
+            raw[s, g] = ps.tile([P, HALF], F32, name="raw_%d_%d" % (s, g), tag="raw%d%d" % (s % 2, g))
             nc.tensor.matmul_mx(out=raw[s, g][:], lhsT=codes["q", h, half][:, cols].bitcast(FP8X4), lhsT_scale=scales["q", h, half][:, cols],
                                 rhs=codes["k", h, g][:].bitcast(FP8X4), rhs_scale=scales["k", h, g][:], start=True, stop=True)
 
         y = {}
 
-        def weigh(s):
+        def weigh(s, g):
             h, block = divmod(s, BLOCKS)
-            y[s] = rotating(sb, "y", Y_BUFS, [P, T], F32, align_bytes=64)
-            parts = [(first, width, level, side, ref_block) for level, first, width, side, ref_block in far_segments(block)]
-            parts.append((block * P, P, None, None, None))
-            for first, width, level, side, ref_block in sorted(parts, key=lambda part: part[0]):
-                g, local = divmod(first, HALF)
+            if g == 0:
+                y[s] = sbuf("y", Y_BUFS, [P, T], F32)
+            parts = far_segments(block) + [(None, block * P, P, None, None)]
+            for row, first, width, side, ref_block in sorted(parts, key=lambda part: part[1]):
+                if first // HALF != g:
+                    continue
                 seg = slice(first, first + width)
-                scores = raw[s, g][:, local : local + width]
-                if level is None:
+                scores = raw[s, g][:, first % HALF : first % HALF + width]
+                if row is None:
                     nc.vector.tensor_tensor(out=y[s][:, seg], in0=scores, in1=diag[h][:, seg], op=ALU.mult)
                 else:
                     n = (block * 2 + side) * BLOCKS + ref_block
                     nc.vector.scalar_tensor_tensor(out=y[s][:, seg], in0=scores, scalar=near[:, h, n : n + 1],
-                                                   in1=far_rows[h][:, level, seg], op0=ALU.mult, op1=ALU.mult)
-            nc.sync.dma_start(out=out_0[h, block * P : (block + 1) * P, :], in_=y[s][:])
+                                                   in1=far_rows[h][:, row, seg], op0=ALU.mult, op1=ALU.mult)
+
+        def store_y(s, cols):
+            h, block = divmod(s, BLOCKS)
+            nc.sync.dma_start(out=out_0[h, block * P : (block + 1) * P, cols], in_=y[s][:, cols])
 
         rounded = {}
 
-        def round_y(s):
-            rounded[s] = rotating(sb, "rounded", 3, [P, T], BF16, align_bytes=64)
-            target = rounded[s][:].rearrange("i (u a e) -> i u a e", u=2, e=2)
-            values = y[s][:].rearrange("i (a u e) -> i u a e", u=2, e=2)
-            if s < STEPS - 1:
+        def round_y(s, engine, first, last):
+            if s not in rounded:
+                rounded[s] = sbuf("rounded", 3, [P, T], BF16)
+            target = rounded[s][:].rearrange("i (u a e) -> i u a e", u=2, e=2)[:, :, first:last, :]
+            values = y[s][:].rearrange("i (a u e) -> i u a e", u=2, e=2)[:, :, first:last, :]
+            if engine == "gpsimd":
                 nc.gpsimd.tensor_scalar(out=target, in0=values, scalar1=1.0, scalar2=1.0, op0=ALU.mult, op1=ALU.mult)
+            elif engine == "vector":
+                vcopy(out=target, in_=values)
             else:
-                nc.vector.tensor_copy(out=target, in_=values)
+                scopy(out=target, in_=values)
 
         group_of = {}
         for h in range(H):
@@ -234,100 +290,160 @@ def tile_bidirectional_decay_scores_g1_kernel(tc, queries, keys, clock, out_0, o
                 first += size
         grouped_out, out_words, out_scales = {}, {}, {}
 
-        def turn_out(s):
-            first, size = group_of[s]
+        turned_out = {}
+
+        def turn_out(s, halves, tag):
             words = rounded[s][:].bitcast(F32)
-            turned = rotating(ps, "turn_out", 2, [P, 2, 2, P], F32)
-            for g in range(2):
+            turned_out[s, halves.start] = psum(tag, 2, [P, 2, 2, P], F32)
+            for g in range(halves.start, halves.stop):
                 for u in range(2):
                     at = 256 * u + P * g
-                    nc.tensor.transpose(turned[:, g, u, :], words[:, at : at + P], ident_f32[:])
-            if s == first:
-                grouped_out[first] = rotating(sb, "grouped_out", 2, [P, 2, 4 * size * P], BF16, align_bytes=64)
+                    nc.tensor.transpose(turned_out[s, halves.start][:, g, u, :], words[:, at : at + P], ident_f32[:])
+
+        def copy_out(s, halves, engine_copy):
+            first, size = group_of[s]
+            if first not in grouped_out:
+                grouped_out[first] = sbuf("grouped_out", 2, [P, 2, 4 * size * P], BF16)
             place = s - first
-            target = grouped_out[first][:, :, 4 * place * P : 4 * (place + 1) * P].bitcast(F32)
-            nc.scalar.copy(out=target.rearrange("k g (r u) -> k g r u", u=2), in_=turned[:].rearrange("k g u r -> k g r u"))
+            target = grouped_out[first][:, halves, 4 * place * P : 4 * (place + 1) * P].bitcast(F32)
+            engine_copy(out=target.rearrange("k g (r u) -> k g r u", u=2),
+                        in_=turned_out[s, halves.start][:, halves, :, :].rearrange("k g u r -> k g r u"))
 
         words_hbm = out_1.rearrange("g p m t -> p g (m t)")
 
-        def quantize_out(first, g):
-            size = group_of[first][1]
-            h, block = divmod(first, BLOCKS)
-            if g == 0:
-                out_words[first] = rotating(sb, "out_words", 3, [P, 2, size * P], U32, align_bytes=64)
-                if block == 0:
-                    out_scales[h] = sb.tile([P, 2, T], U8, name="out_scales%d" % h, align_bytes=64)
-            nc.vector.quantize_mx(out=out_words[first][:, g, :].bitcast(FP8X4),
-                                  scales=out_scales[h][:, g, block * P : (block + size) * P], in_=grouped_out[first][:, g, :])
-            if g == 1:
-                nc.sync.dma_start(out=words_hbm[:, :, 4 * first * P : 4 * (first + size) * P].bitcast(I32),
-                                  in_=out_words[first][:].bitcast(I32))
-                if block + size == BLOCKS:
-                    for quad in range(4):
-                        nc.sync.dma_start(
-                            out=out_2[:, 4 * quad : 4 * quad + 4, h * T : (h + 1) * T].rearrange("g r m -> r g m").bitcast(I32),
-                            in_=out_scales[h][32 * quad : 32 * quad + 4, :, :].bitcast(I32))
+        def store_words(halves, first, blocks, words):
+            nc.sync.dma_start(out=words_hbm[:, halves, 4 * first * P : 4 * (first + blocks) * P].bitcast(I32), in_=words.bitcast(I32))
 
-        vcopy, scopy = nc.vector.tensor_copy, nc.scalar.copy
-        turn_in("k", 0, 0, 0, vcopy)
+        def quantize_out(start, blocks, g, words):
+            first = group_of[start][0]
+            h, block = divmod(start, BLOCKS)
+            if h not in out_scales:
+                out_scales[h] = sbuf("out_scales", H, [P, 2, T], U8)
+            place = start - first
+            nc.vector.quantize_mx(out=words.bitcast(FP8X4), scales=out_scales[h][:, g, block * P : (block + blocks) * P],
+                                  in_=grouped_out[first][:, g, 4 * place * P : 4 * (place + blocks) * P])
+
+        def store_scales(h):
+            for quad in range(4):
+                nc.sync.dma_start(
+                    out=out_2[:, 4 * quad : 4 * quad + 4, h * T : (h + 1) * T].rearrange("g r m -> r g m").bitcast(I32),
+                    in_=out_scales[h][32 * quad : 32 * quad + 4, :, :].bitcast(I32))
+
+        def finish_half(first, g):
+            size = group_of[first][1]
+            words = sbuf("out_words", 4, [P, 1, size * P], U32)
+            quantize_out(first, size, g, words[:, 0, :])
+            store_words(slice(g, g + 1), first, size, words[:])
+            if (first + size) % BLOCKS == 0 and g == 1:
+                store_scales(first // BLOCKS)
+
+        both = slice(0, 2)
+        turn_in("k", 0, 0, 0)
+        copy_in("k", 0, 0, 0, vcopy)
         spread_clock(0)
         keep_clock(0, scopy)
-        turn_in("k", 0, 0, 1, vcopy)
-        block_job(0)
-        turn_in("q", 0, 0, 0, vcopy)
+        turn_in("k", 0, 0, 1)
+        copy_in("k", 0, 0, 1, vcopy)
+        turn_in("q", 0, 0, 0, "raw01")
+        copy_in("q", 0, 0, 0, vcopy)
+        run_jobs(-1, 896, 0)
         quantize_in("k", 0, 0, 0, 2)
-        turn_in("k", 0, 1, 0, vcopy)
+        turn_in("k", 0, 1, 0, "raw11")
+        copy_in("k", 0, 1, 0, scopy)
         quantize_in("q", 0, 0, 0, 1)
+        turn_in("k", 0, 1, 1)
+        copy_in("k", 0, 1, 1, scopy)
+        turn_in("q", 0, 0, 1)
         multiply(0, 0)
-        turn_in("k", 0, 1, 1, scopy)
-        block_job(1)
-        turn_in("q", 0, 0, 1, vcopy)
+        multiply(1, 0)
+        turn_in("q", 0, 1, 0, "turn_out0")
+        turn_in("q", 0, 1, 1, "turn_out1")
+        run_jobs(0, 1280, 0)
+        copy_in("q", 0, 0, 1, scopy)
+        run_jobs(1, 0, 0)
+        weigh(0, 0)
         quantize_in("k", 0, 1, 0, 2)
         multiply(0, 1)
+        multiply(1, 1)
+        weigh(1, 0)
         quantize_in("q", 0, 0, 1, 1)
+        copy_in("q", 0, 1, 0, scopy)
+        copy_in("q", 0, 1, 1, scopy)
+        ahead = done[1]
 
-        units = [("q", 0, 1, 0), ("q", 0, 1, 1)]
+        units = []
         for h in range(1, H):
             for which, half in (("k", 0), ("k", 1), ("q", 0), ("q", 1)):
                 units.extend([(which, h, half, 0), (which, h, half, 1)])
-        units_at = {0: units[0:2], 1: units[2:4]}
-        for n in range(4, len(units)):
-            units_at[n - 2] = [units[n]]
+        on_vector = (1,5)
         quant_at = {}
-        for s, listed in units_at.items():
-            if listed[-1][3] == 1:
-                quant_at[s + 1] = [("in",) + listed[-1][0:3]]
-        for first in range(0, 24, 4):
-            quant_at[first + 7] = [("out", first, 0)]
-            quant_at[first + 9] = [("out", first, 1)]
-        quant_at[30] = [("out", 24, 0)]
-        quant_at[31] = [("out", 24, 1)]
-        quant_at[32] = [("out", 28, 0), ("out", 28, 1)]
-        quant_at[33] = [("out", 30, 0), ("out", 30, 1)]
-        quant_at[34] = [("out", 31, 0), ("out", 31, 1)]
+        for n in range(1, len(units), 2):
+            quant_at[n + 1] = (quantize_in, units[n][0:3] + (0, 2))
+        quant_at[3] = quant_at[2]
+        quant_at[2] = (quantize_in, ("q", 0, 1, 0, 2))
+        for first in range(0, 20, 4):
+            quant_at[first + 7] = (finish_half, (first, 0))
+            quant_at[first + 9] = (finish_half, (first, 1))
+        quant_at[26] = (finish_half, (20, 0))
+        quant_at[27] = (finish_half, (20, 1))
+        quant_at[28] = (finish_half, (24, 0))
+        quant_at[29] = (finish_half, (24, 1))
+        quant_at[30] = (finish_half, (26, 0))
+        turn_in(*units[0])
+        shares = {0: 200, 1: 128, 5: 240,9:248,13:248,17:248,21:248}
 
-        for s in range(STEPS + 3):
-            if s + 1 < STEPS:
+        def split(s):
+            return shares.get(s, 192)
+
+        for s in range(STEPS):
+            if s < len(units) and s not in on_vector:
+                copy_in(*units[s], scopy)
+            if 0 < s < STEPS - 1:
+                round_y(s - 1, "scalar", 0, 256 - split(s - 1))
+            if s >= 3:
+                copy_out(s - 3, both, vcopy if s in (10,14,18,22) else scopy)
+            if 0 < s < STEPS - 1:
                 multiply(s + 1, 0)
                 multiply(s + 1, 1)
-            if s + 2 < STEPS:
-                block_job(s + 2)
-            for which, h, half, b in units_at.get(s, []):
-                turn_in(which, h, half, b, scopy)
-            if 2 <= s < STEPS + 2:
-                turn_out(s - 2)
-            if s < STEPS:
-                weigh(s)
-            if s % BLOCKS == 3 and s + BLOCKS < STEPS:
-                spread_clock(s // BLOCKS + 1)
-            if s % BLOCKS == 4 and s + BLOCKS < STEPS:
-                keep_clock(s // BLOCKS + 1, vcopy)
-            if s < STEPS - 1:
-                round_y(s)
-            for job in quant_at.get(s, []):
-                if job[0] == "in":
-                    quantize_in(job[1], job[2], job[3], 0, 2)
-                else:
-                    quantize_out(job[1], job[2])
+            if s >= 2:
+                turn_out(s - 2, both, "turn_out")
+            if s + 1 < len(units):
+                turn_in(*units[s + 1])
+            run_jobs(s + 2, ahead + min(per_step + 0, per_step + 0 // (s + 1)) * (s + 1), (s + 5) // BLOCKS)
             if s == STEPS - 1:
-                round_y(s)
+                break
+            if s > 1:
+                weigh(s, 0)
+            weigh(s, 1)
+            store_y(s, slice(0, T))
+            round_y(s, "gpsimd", 256 - split(s), 256)
+            if s in on_vector:
+                copy_in(*units[s], vcopy)
+            if s in quant_at:
+                quant_at[s][0](*quant_at[s][1])
+
+        last = STEPS - 1
+        weigh(last, 0)
+        store_y(last, slice(0, HALF))
+        round_y(last - 1, "scalar", 0, 256 - split(last - 1))
+        round_y(last, "scalar", 0, P)
+        copy_out(last - 2, both, scopy)
+        weigh(last, 1)
+        store_y(last, slice(HALF, T))
+        finish_half(last - 5, 1)
+        round_y(last, "vector", P, 256)
+        turn_out(last - 1, both, "turn_out")
+        turn_out(last, slice(0, 1), "turn_in")
+        turn_out(last, slice(1, 2), "turn_in")
+        before = sbuf("out_words", 4, [P, 2, 2 * P], U32)
+        quantize_out(last - 3, 2, 0, before[:, 0, :])
+        quantize_out(last - 3, 2, 1, before[:, 1, :])
+        store_words(both, last - 3, 2, before[:])
+        copy_out(last - 1, both, scopy)
+        copy_out(last, slice(0, 1), vcopy)
+        copy_out(last, slice(1, 2), scopy)
+        final = sbuf("out_words", 4, [P, 2, 2 * P], U32)
+        quantize_out(last - 1, 2, 0, final[:, 0, :])
+        quantize_out(last - 1, 2, 1, final[:, 1, :])
+        store_words(both, last - 1, 2, final[:])
+        store_scales(H - 1)

@@ -22,7 +22,7 @@ UNIT = 256
 HALF = 512
 START, END = 0, 1
 Y_BUFS = 10
-WARM = 12
+WARM = 8
 GROUPS = [[4, 4], [4, 4], [4, 4], [2, 2, 2, 2]]
 ROWS = 2
 
@@ -63,28 +63,32 @@ def tile_bidirectional_decay_scores_g1_kernel(tc, queries, keys, clock, out_0, o
 
         def load_unit(which, h, half, b):
             if b == 0:
-                raw_in[which, h, half] = sbuf("raw_in", 4 * H, [P, 2, 2 * DK], BF16)
+                raw_in[which, h, half] = sbuf("raw_in", 4, [P, 2, 2 * DK], BF16)
             first = half * HALF + b * UNIT
             nc.sync.dma_start(out=raw_in[which, h, half][:, b, :],
                               in_=source[which][h, first : first + UNIT, :].rearrange("(p j) c -> p (j c)", j=2))
 
         def load_half(which, h, half):
-            raw_in[which, h, half] = sbuf("raw_in", 4 * H, [P, 2, 2 * DK], BF16)
+            raw_in[which, h, half] = sbuf("raw_in", 4, [P, 2, 2 * DK], BF16)
             nc.sync.dma_start(out=raw_in[which, h, half][:].rearrange("p b x -> p (b x)"),
                               in_=source[which][h, half * HALF : (half + 1) * HALF, :].rearrange("(p j) c -> p (j c)", j=4))
 
         clock_rows = sbuf("clock_rows", 1, [P, P], BF16)
         nc.sync.dma_start(out=clock_rows[0:STEPS, :], in_=clock.rearrange("h (b p) -> (h b) p", p=P))
+        clock_pairs = sbuf("clock_pairs", 1, [P, 2 * P], BF16)
+        nc.vector.memset(clock_pairs[:].bitcast(F32), 0.0)
+        nc.sync.dma_start(out=clock_pairs[0 : STEPS // 2, :], in_=clock.rearrange("h (b p) -> (h b) p", p=2 * P))
         by_units = [("k", 0, 0), ("q", 0, 0), ("k", 0, 1)]
         for which, h, half, b in (("k", 0, 0, 0), ("k", 0, 0, 1), ("q", 0, 0, 0), ("k", 0, 1, 0), ("k", 0, 1, 1), ("q", 0, 0, 1)):
             load_unit(which, h, half, b)
         load_half("q", 0, 1)
-        later_clocks = sbuf("later_clocks", 1, [P, (H - 1) * T], BF16)
         for h in range(1, H):
-            for which, half in (("k", 0), ("k", 1), ("q", 0), ("q", 1)):
-                load_half(which, h, half)
-                if (h, which, half) == (1, "k", 1):
-                    nc.sync.dma_start(out=later_clocks[:], in_=clock[1:H, :].rearrange("h t -> (h t)").partition_broadcast(P))
+            for which in ("k", "q"):
+                whole = sbuf("raw_whole", 2 * (H - 1), [P, 2, 2, 2 * DK], BF16)
+                nc.sync.dma_start(out=whole[:].rearrange("p a b x -> p a (b x)"),
+                                  in_=source[which][h, :, :].rearrange("(a p j) c -> p a (j c)", a=2, j=4))
+                for half in range(2):
+                    raw_in[which, h, half] = whole[:, half, :, :]
 
         table_warm = sbuf("table_warm", 1, [P, 1], F32)
         ones = sbuf("ones", 1, [P, 4 * P], BF16)
@@ -112,6 +116,10 @@ def tile_bidirectional_decay_scores_g1_kernel(tc, queries, keys, clock, out_0, o
         nc.tensor.transpose(bank[:, 0, :], clock_rows[:], ident_bf[:])
         nc.tensor.transpose(bank[:, 1, :], clock_rows[:, 0:1].to_broadcast([P, P]), ident_bf[:])
         nc.tensor.transpose(bank[:, 2, :], clock_rows[:, P - 1 : P].to_broadcast([P, P]), ident_bf[:])
+        pair_bank = psum("turn_out", 2, [P, P], F32)
+        nc.tensor.transpose(pair_bank[:], clock_pairs[:].bitcast(F32), ident_f32[:])
+        pair_cols = sbuf("pair_cols", 1, [P, STEPS // 2], F32)
+        vcopy(out=pair_cols[:], in_=pair_bank[:, 0 : STEPS // 2])
         marks = sbuf("marks", 1, [P, 3, STEPS], BF16)
         vcopy(out=marks[:], in_=bank[:, :, 0:STEPS])
         neg_end = sbuf("neg_end", 1, [P, STEPS], F32)
@@ -127,18 +135,16 @@ def tile_bidirectional_decay_scores_g1_kernel(tc, queries, keys, clock, out_0, o
                 op=ALU.subtract)
 
         clock_wide, wide_banks = {}, {}
-        for h in range(1, H):
-            clock_wide[h] = later_clocks[:, (h - 1) * T : h * T]
 
-        def spread_clock(h):
-            wide_banks[h] = psum("turn_out", 2, [P, T], BF16)
-            for b in range(BLOCKS):
-                n = h * BLOCKS + b
-                nc.tensor.transpose(wide_banks[h][:, b * P : (b + 1) * P], marks[:, 0, n : n + 1].to_broadcast([P, P]), ident_bf[:])
+        def spread_clock(h, tag):
+            wide_banks[h] = ps.tile([P, 4, P], F32, name="wide_%d" % h, tag=tag)
+            for b in range(4):
+                n = 4 * h + b
+                nc.tensor.transpose(wide_banks[h][:, b, :], pair_cols[:, n : n + 1].to_broadcast([P, P]), ident_f32[:])
 
         def keep_clock(h, engine_copy):
-            clock_wide[h] = sbuf("clock_wide", 1, [P, T], BF16)[:]
-            engine_copy(out=clock_wide[h][:], in_=wide_banks[h][:])
+            clock_wide[h] = sbuf("clock_wide", H, [P, T], BF16)
+            engine_copy(out=clock_wide[h][:].bitcast(F32), in_=wide_banks[h][:].rearrange("p b x -> p (b x)"))
 
         far_rows, diag, dist, gaps_abs = {}, {}, {}, {}
 
@@ -244,12 +250,14 @@ def tile_bidirectional_decay_scores_g1_kernel(tc, queries, keys, clock, out_0, o
             nc.tensor.matmul_mx(out=raw[s, g][:], lhsT=codes["q", h, half][:, cols].bitcast(FP8X4), lhsT_scale=scales["q", h, half][:, cols],
                                 rhs=codes["k", h, g][:].bitcast(FP8X4), rhs_scale=scales["k", h, g][:], start=True, stop=True)
 
-        y = {}
+        y, y_pair = {}, {}
 
         def weigh(s, g):
             h, block = divmod(s, BLOCKS)
             if g == 0:
-                y[s] = sbuf("y", Y_BUFS, [P, T], F32)
+                if s % 2 == 0:
+                    y_pair[s] = sbuf("y", Y_BUFS // 2, [P, 2, T], F32)
+                y[s] = y_pair[s - s % 2][:, s % 2, :]
             parts = far_segments(block) + [(None, block * P, P, None, None)]
             for row, first, width, side, ref_block in sorted(parts, key=lambda part: part[1]):
                 if first // HALF != g:
@@ -324,48 +332,55 @@ def tile_bidirectional_decay_scores_g1_kernel(tc, queries, keys, clock, out_0, o
                                   in_=grouped_out[first][:, g, 4 * place * P : 4 * (place + blocks) * P])
 
         def store_scales(h):
-            for quad in range(4):
+            for r in range(4):
                 nc.sync.dma_start(
-                    out=out_2[:, 4 * quad : 4 * quad + 4, h * T : (h + 1) * T].rearrange("g r m -> r g m").bitcast(I32),
-                    in_=out_scales[h][32 * quad : 32 * quad + 4, :, :].bitcast(I32))
+                    out=out_2[:, r:16:4, h * T : (h + 1) * T].rearrange("g q m -> q g m").bitcast(I32),
+                    in_=out_scales[h][r:P:32, :, :].bitcast(I32))
 
         def finish_half(first, g):
             size = group_of[first][1]
-            words = sbuf("out_words", 4, [P, 1, size * P], U32)
-            quantize_out(first, size, g, words[:, 0, :])
-            store_words(slice(g, g + 1), first, size, words[:])
-            if (first + size) % BLOCKS == 0 and g == 1:
-                store_scales(first // BLOCKS)
+            if g == 0:
+                out_words[first] = sbuf("out_words", 3, [P, 2, size * P], U32)
+            quantize_out(first, size, g, out_words[first][:, g, :])
+            if g == 1:
+                store_words(slice(0, 2), first, size, out_words[first][:])
+                if (first + size) % BLOCKS == 0:
+                    store_scales(first // BLOCKS)
 
         both = slice(0, 2)
         turn_in("k", 0, 0, 0)
+        spread_clock(0, "raw10")
         copy_in("k", 0, 0, 0, vcopy)
-        spread_clock(0)
         keep_clock(0, scopy)
         turn_in("k", 0, 0, 1)
+        spread_clock(1, "raw00")
         copy_in("k", 0, 0, 1, vcopy)
         turn_in("q", 0, 0, 0, "raw01")
         copy_in("q", 0, 0, 0, vcopy)
         run_jobs(-1, 896, 0)
+        keep_clock(1, scopy)
         quantize_in("k", 0, 0, 0, 2)
         turn_in("k", 0, 1, 0, "raw11")
+        spread_clock(2, "turn_out0")
+        spread_clock(3, "turn_out1")
         copy_in("k", 0, 1, 0, scopy)
         quantize_in("q", 0, 0, 0, 1)
         turn_in("k", 0, 1, 1)
         copy_in("k", 0, 1, 1, scopy)
-        turn_in("q", 0, 0, 1)
+        keep_clock(2, vcopy)
         multiply(0, 0)
         multiply(1, 0)
+        turn_in("q", 0, 0, 1)
         turn_in("q", 0, 1, 0, "turn_out0")
-        turn_in("q", 0, 1, 1, "turn_out1")
-        run_jobs(0, 1280, 0)
-        copy_in("q", 0, 0, 1, scopy)
         run_jobs(1, 0, 0)
         weigh(0, 0)
         quantize_in("k", 0, 1, 0, 2)
+        copy_in("q", 0, 0, 1, scopy)
         multiply(0, 1)
         multiply(1, 1)
+        keep_clock(3, vcopy)
         weigh(1, 0)
+        turn_in("q", 0, 1, 1, "turn_out1")
         quantize_in("q", 0, 0, 1, 1)
         copy_in("q", 0, 1, 0, scopy)
         copy_in("q", 0, 1, 1, scopy)
@@ -376,19 +391,13 @@ def tile_bidirectional_decay_scores_g1_kernel(tc, queries, keys, clock, out_0, o
             for which, half in (("k", 0), ("k", 1), ("q", 0), ("q", 1)):
                 units.extend([(which, h, half, 0), (which, h, half, 1)])
         on_vector = (1,5)
+        halves_in = [("q", 0, 1)] + [unit[0:3] for unit in units[0::2]]
         quant_at = {}
-        for n in range(1, len(units), 2):
-            quant_at[n + 1] = (quantize_in, units[n][0:3] + (0, 2))
-        quant_at[3] = quant_at[2]
-        quant_at[2] = (quantize_in, ("q", 0, 1, 0, 2))
-        for first in range(0, 20, 4):
-            quant_at[first + 7] = (finish_half, (first, 0))
-            quant_at[first + 9] = (finish_half, (first, 1))
-        quant_at[26] = (finish_half, (20, 0))
-        quant_at[27] = (finish_half, (20, 1))
-        quant_at[28] = (finish_half, (24, 0))
-        quant_at[29] = (finish_half, (24, 1))
-        quant_at[30] = (finish_half, (26, 0))
+        for step, half in zip((2,3,4,6,8,10,12,14,16,18,20,22,24), halves_in):
+            quant_at[step] = (quantize_in, half + (0, 2))
+        outs = [(first, g) for first in (0,4,8,12,16,20,24,26) for g in range(2)]
+        for step, out in zip((7,9,11,13,15,17,19,21,23,25,26,27,28,29,30), outs):
+            quant_at[step] = (finish_half, out)
         turn_in(*units[0])
         shares = {0: 200, 1: 128, 5: 240,9:248,13:248,17:248,21:248}
 
@@ -409,13 +418,17 @@ def tile_bidirectional_decay_scores_g1_kernel(tc, queries, keys, clock, out_0, o
                 turn_out(s - 2, both, "turn_out")
             if s + 1 < len(units):
                 turn_in(*units[s + 1])
-            run_jobs(s + 2, ahead + min(per_step + 0, per_step + 0 // (s + 1)) * (s + 1), (s + 5) // BLOCKS)
+            run_jobs(s + 2, ahead + min(per_step + 0, per_step + 0 // (s + 1)) * (s + 1), H)
             if s == STEPS - 1:
                 break
             if s > 1:
                 weigh(s, 0)
             weigh(s, 1)
-            store_y(s, slice(0, T))
+            if s >= 20:
+                store_y(s, slice(0, T))
+            elif s % 2 == 1:
+                h, block = divmod(s - 1, BLOCKS)
+                nc.sync.dma_start(out=out_0[h, block * P : (block + 2) * P, :].rearrange("(b p) j -> p b j", b=2), in_=y_pair[s - 1][:])
             round_y(s, "gpsimd", 256 - split(s), 256)
             if s in on_vector:
                 copy_in(*units[s], vcopy)
@@ -435,14 +448,14 @@ def tile_bidirectional_decay_scores_g1_kernel(tc, queries, keys, clock, out_0, o
         turn_out(last - 1, both, "turn_out")
         turn_out(last, slice(0, 1), "turn_in")
         turn_out(last, slice(1, 2), "turn_in")
-        before = sbuf("out_words", 4, [P, 2, 2 * P], U32)
+        before = sbuf("out_words", 3, [P, 2, 2 * P], U32)
         quantize_out(last - 3, 2, 0, before[:, 0, :])
         quantize_out(last - 3, 2, 1, before[:, 1, :])
         store_words(both, last - 3, 2, before[:])
         copy_out(last - 1, both, scopy)
         copy_out(last, slice(0, 1), vcopy)
         copy_out(last, slice(1, 2), scopy)
-        final = sbuf("out_words", 4, [P, 2, 2 * P], U32)
+        final = sbuf("out_words", 3, [P, 2, 2 * P], U32)
         quantize_out(last - 1, 2, 0, final[:, 0, :])
         quantize_out(last - 1, 2, 1, final[:, 1, :])
         store_words(both, last - 1, 2, final[:])

@@ -18,22 +18,20 @@ ACT = mybir.ActivationFunctionType
 P = 128
 BLOCKS = T // P
 STEPS = H * BLOCKS
-UNIT = 256
 HALF = 512
+UNIT = 256
+WORDS = T // 4
 START, END = 0, 1
-Y_BUFS = 10
-WARM = 8
+
+Y_SLOTS = 10
 GROUPS = [[4, 4], [4, 4], [4, 4], [2, 2, 2, 2]]
-ROWS = 2
-
-
-def far_segments(block):
-    found = []
-    for other in range(BLOCKS):
-        if other != block:
-            side = START if other > block else END
-            found.append((side, other * P, P, side, other))
-    return found
+GPSIMD_WORDS = 208
+GPSIMD_WORDS_AT = {0: 200, 1: 128, 5: 240, 11: 248, 19: 248}
+COPY_IN_ON_VECTOR = (1, 5)
+COPY_OUT_ON_VECTOR = (12, 20)
+QUANTIZE_IN_STEPS = (2, 3) + tuple(range(4, 25, 2))
+QUANTIZE_OUT_STEPS = tuple(range(7, 26, 2)) + (26, 27, 28, 29, 30)
+WARM_PASSES = 8
 
 
 def tile_bidirectional_decay_scores_g1_kernel(tc, queries, keys, clock, out_0, out_1, out_2):
@@ -43,56 +41,54 @@ def tile_bidirectional_decay_scores_g1_kernel(tc, queries, keys, clock, out_0, o
         ps = ctx.enter_context(tc.psum_pool(name="ps", bufs=1))
         ctx.enter_context(tc.manual_schedule())
 
-        counters = {}
+        taken = {}
 
-        def slot(tag, slots):
-            n = counters.get(tag, 0)
-            counters[tag] = n + 1
-            return dict(name="%s_%d" % (tag, n), tag="%s%d" % (tag, n % slots))
+        def next_slot(family, slots):
+            n = taken.get(family, 0)
+            taken[family] = n + 1
+            return dict(name="%s_%d" % (family, n), tag="%s%d" % (family, n % slots))
 
-        def sbuf(tag, slots, shape, dtype):
-            return sb.tile(shape, dtype, align_bytes=64, **slot(tag, slots))
+        def sbuf(family, slots, shape, dtype):
+            return sb.tile(shape, dtype, align_bytes=64, **next_slot(family, slots))
 
-        def psum(tag, slots, shape, dtype):
-            return ps.tile(shape, dtype, **slot(tag, slots))
+        def rotating_bank(family, shape, dtype):
+            return ps.tile(shape, dtype, **next_slot(family, 2))
 
-        vcopy, scopy = nc.vector.tensor_copy, nc.scalar.copy
+        def named_bank(tag, name, shape, dtype):
+            return ps.tile(shape, dtype, name=name, tag=tag)
+
+        vector_copy, scalar_copy = nc.vector.tensor_copy, nc.scalar.copy
+        both = slice(0, 2)
 
         source = {"q": queries, "k": keys}
         raw_in = {}
-
-        def load_unit(which, h, half, b):
-            if b == 0:
-                raw_in[which, h, half] = sbuf("raw_in", 4, [P, 2, 2 * DK], BF16)
-            first = half * HALF + b * UNIT
-            nc.sync.dma_start(out=raw_in[which, h, half][:, b, :],
-                              in_=source[which][h, first : first + UNIT, :].rearrange("(p j) c -> p (j c)", j=2))
-
-        def load_half(which, h, half):
-            raw_in[which, h, half] = sbuf("raw_in", 4, [P, 2, 2 * DK], BF16)
-            nc.sync.dma_start(out=raw_in[which, h, half][:].rearrange("p b x -> p (b x)"),
-                              in_=source[which][h, half * HALF : (half + 1) * HALF, :].rearrange("(p j) c -> p (j c)", j=4))
+        by_units = [("k", 0, 0), ("q", 0, 0), ("k", 0, 1)]
 
         clock_rows = sbuf("clock_rows", 1, [P, P], BF16)
         nc.sync.dma_start(out=clock_rows[0:STEPS, :], in_=clock.rearrange("h (b p) -> (h b) p", p=P))
         clock_pairs = sbuf("clock_pairs", 1, [P, 2 * P], BF16)
-        nc.vector.memset(clock_pairs[:].bitcast(F32), 0.0)
-        nc.sync.dma_start(out=clock_pairs[0 : STEPS // 2, :], in_=clock.rearrange("h (b p) -> (h b) p", p=2 * P))
-        by_units = [("k", 0, 0), ("q", 0, 0), ("k", 0, 1)]
-        for which, h, half, b in (("k", 0, 0, 0), ("k", 0, 0, 1), ("q", 0, 0, 0), ("k", 0, 1, 0), ("k", 0, 1, 1), ("q", 0, 0, 1)):
-            load_unit(which, h, half, b)
-        load_half("q", 0, 1)
+        for part in range(2):
+            nc.scalar.dma_start(out=clock_pairs[16 * part : 16 * part + 16, :], in_=clock.rearrange("h (b p) -> (h b) p", p=2 * P))
+        for which, h, half, unit in (("k", 0, 0, 0), ("k", 0, 0, 1), ("q", 0, 0, 0), ("k", 0, 1, 0), ("k", 0, 1, 1), ("q", 0, 0, 1)):
+            if unit == 0:
+                raw_in[which, h, half] = sbuf("raw_half", 4, [P, 2, 2 * DK], BF16)
+            first = half * HALF + unit * UNIT
+            nc.sync.dma_start(out=raw_in[which, h, half][:, unit, :],
+                              in_=source[which][h, first : first + UNIT, :].rearrange("(p j) c -> p (j c)", j=2))
+        raw_in["q", 0, 1] = sbuf("raw_half", 4, [P, 2, 2 * DK], BF16)
+        nc.sync.dma_start(out=raw_in["q", 0, 1][:].rearrange("p b x -> p (b x)"),
+                          in_=queries[0, HALF:T, :].rearrange("(p j) c -> p (j c)", j=4))
         for h in range(1, H):
             for which in ("k", "q"):
-                whole = sbuf("raw_whole", 2 * (H - 1), [P, 2, 2, 2 * DK], BF16)
+                whole = sbuf("raw_head", 2 * (H - 1), [P, 2, 2, 2 * DK], BF16)
                 nc.sync.dma_start(out=whole[:].rearrange("p a b x -> p a (b x)"),
                                   in_=source[which][h, :, :].rearrange("(a p j) c -> p a (j c)", a=2, j=4))
                 for half in range(2):
                     raw_in[which, h, half] = whole[:, half, :, :]
 
-        table_warm = sbuf("table_warm", 1, [P, 1], F32)
         ones = sbuf("ones", 1, [P, 4 * P], BF16)
         nc.vector.memset(ones[:].bitcast(F32), 1.0)
+        table_warm = sbuf("table_warm", 1, [P, 1], F32)
         nc.scalar.activation(out=table_warm[:], in_=ones[:, 0:1], func=ACT.Exp)
         ident_bf = sbuf("ident_bf", 1, [P, P], BF16)
         ident_f32 = sbuf("ident_f32", 1, [P, P], F32)
@@ -101,31 +97,27 @@ def tile_bidirectional_decay_scores_g1_kernel(tc, queries, keys, clock, out_0, o
         warm_codes = sbuf("warm_codes", 1, [P, P], U32)
         warm_scales = sbuf("warm_scales", 1, [P, P], U8)
         nc.vector.quantize_mx(out=warm_codes[:].bitcast(FP8X4), scales=warm_scales[:], in_=ones[:])
-        nc.vector.memset(clock_rows[32:64, :], 0.0)
-        nc.vector.memset(clock_rows[64:P, :], 0.0)
+        for tile in (clock_rows, clock_pairs):
+            nc.vector.memset(tile[32:64, :], 0.0)
+            nc.vector.memset(tile[64:P, :], 0.0)
+        warm_bank = named_bank("scores00", "warm_bank", [P, 4, P], F32)
+        for n in range(WARM_PASSES):
+            nc.tensor.matmul_mx(out=warm_bank[:, n % 4, :], lhsT=warm_codes[:].bitcast(FP8X4), lhsT_scale=warm_scales[:],
+                                rhs=warm_codes[:].bitcast(FP8X4), rhs_scale=warm_scales[:], start=True, stop=True)
 
-        def warm(count):
-            bank = ps.tile([P, HALF], F32, name="warm_bank", tag="raw00")
-            for n in range(count):
-                nc.tensor.matmul_mx(out=bank[:, n % 4 * P : (n % 4 + 1) * P], lhsT=warm_codes[:].bitcast(FP8X4), lhsT_scale=warm_scales[:],
-                                    rhs=warm_codes[:].bitcast(FP8X4), rhs_scale=warm_scales[:], start=True, stop=True)
-
-        warm(WARM)
-
-        bank = psum("turn_out", 2, [P, 3, P], BF16)
-        nc.tensor.transpose(bank[:, 0, :], clock_rows[:], ident_bf[:])
-        nc.tensor.transpose(bank[:, 1, :], clock_rows[:, 0:1].to_broadcast([P, P]), ident_bf[:])
-        nc.tensor.transpose(bank[:, 2, :], clock_rows[:, P - 1 : P].to_broadcast([P, P]), ident_bf[:])
-        pair_bank = psum("turn_out", 2, [P, P], F32)
+        marks_bank = rotating_bank("turn_out", [P, 3, P], BF16)
+        nc.tensor.transpose(marks_bank[:, 0, :], clock_rows[:], ident_bf[:])
+        nc.tensor.transpose(marks_bank[:, 1 + START, :], clock_rows[:, 0:1].to_broadcast([P, P]), ident_bf[:])
+        nc.tensor.transpose(marks_bank[:, 1 + END, :], clock_rows[:, P - 1 : P].to_broadcast([P, P]), ident_bf[:])
+        pair_bank = rotating_bank("turn_out", [P, P], F32)
         nc.tensor.transpose(pair_bank[:], clock_pairs[:].bitcast(F32), ident_f32[:])
         pair_cols = sbuf("pair_cols", 1, [P, STEPS // 2], F32)
-        vcopy(out=pair_cols[:], in_=pair_bank[:, 0 : STEPS // 2])
+        vector_copy(out=pair_cols[:], in_=pair_bank[:, 0 : STEPS // 2])
         marks = sbuf("marks", 1, [P, 3, STEPS], BF16)
-        vcopy(out=marks[:], in_=bank[:, :, 0:STEPS])
+        vector_copy(out=marks[:], in_=marks_bank[:, :, 0:STEPS])
         neg_end = sbuf("neg_end", 1, [P, STEPS], F32)
-        nc.gpsimd.tensor_scalar(out=neg_end[:], in0=marks[:, 2, :], scalar1=-1.0, scalar2=1.0, op0=ALU.mult, op1=ALU.mult)
+        nc.gpsimd.tensor_scalar(out=neg_end[:], in0=marks[:, 1 + END, :], scalar1=-1.0, scalar2=1.0, op0=ALU.mult, op1=ALU.mult)
         gaps = sbuf("gaps", 1, [P, H, BLOCKS, 2, BLOCKS], F32)
-        near = sbuf("near", 1, [P, H, BLOCKS * 2 * BLOCKS], F32)
         for h in range(H):
             blocks = slice(h * BLOCKS, (h + 1) * BLOCKS)
             nc.gpsimd.tensor_tensor(
@@ -134,160 +126,153 @@ def tile_bidirectional_decay_scores_g1_kernel(tc, queries, keys, clock, out_0, o
                 in1=marks[:, 1:3, blocks].unsqueeze(1).to_broadcast([P, BLOCKS, 2, BLOCKS]),
                 op=ALU.subtract)
 
-        clock_wide, wide_banks = {}, {}
+        clock_wide, wide_bank = {}, {}
 
         def spread_clock(h, tag):
-            wide_banks[h] = ps.tile([P, 4, P], F32, name="wide_%d" % h, tag=tag)
+            wide_bank[h] = named_bank(tag, "wide_%d" % h, [P, 4, P], F32)
             for b in range(4):
-                n = 4 * h + b
-                nc.tensor.transpose(wide_banks[h][:, b, :], pair_cols[:, n : n + 1].to_broadcast([P, P]), ident_f32[:])
+                column = pair_cols[:, 4 * h + b : 4 * h + b + 1]
+                nc.tensor.transpose(wide_bank[h][:, b, :], column.to_broadcast([P, P]), ident_f32[:])
 
-        def keep_clock(h, engine_copy):
+        def keep_clock(h, copy):
             clock_wide[h] = sbuf("clock_wide", H, [P, T], BF16)
-            engine_copy(out=clock_wide[h][:].bitcast(F32), in_=wide_banks[h][:].rearrange("p b x -> p (b x)"))
+            copy(out=clock_wide[h][:].bitcast(F32), in_=wide_bank[h][:].rearrange("p b x -> p (b x)"))
 
-        far_rows, diag, dist, gaps_abs = {}, {}, {}, {}
+        query_factor = sbuf("query_factor", 1, [P, H, BLOCKS * 2 * BLOCKS], F32)
+        key_factor, diagonal, distance, abs_gaps = {}, {}, {}, {}
 
         def job_open_head(h):
-            far_rows[h] = sbuf("far_rows", 2, [P, ROWS, T], F32)
-            diag[h] = sbuf("diag", 2, [P, T], F32)
-            gaps_abs[h] = sbuf("gaps_abs", 2, [P, BLOCKS * 2 * BLOCKS], F32)
-            nc.scalar.activation(out=gaps_abs[h][:], in_=gaps[:, h, :, :, :].rearrange("p i e j -> p (i e j)"), func=ACT.Abs)
+            key_factor[h] = sbuf("key_factor", 2, [P, 2, T], F32)
+            diagonal[h] = sbuf("diagonal", 2, [P, T], F32)
+            abs_gaps[h] = sbuf("abs_gaps", 2, [P, BLOCKS * 2 * BLOCKS], F32)
+            nc.scalar.activation(out=abs_gaps[h][:], in_=gaps[:, h, :, :, :].rearrange("p i e j -> p (i e j)"), func=ACT.Abs)
 
-        def job_near(h):
-            nc.scalar.activation(out=near[:, h, :], in_=gaps_abs[h][:], func=ACT.Exp, scale=-1.0)
+        def job_query_factor(h):
+            nc.scalar.activation(out=query_factor[:, h, :], in_=abs_gaps[h][:], func=ACT.Exp, scale=-1.0)
 
-        def job_dist(s):
+        def job_distance(s):
             h, block = divmod(s, BLOCKS)
-            dist[s] = sbuf("dist", 3, [P, P], F32)
-            nc.scalar.activation(out=dist[s][:], in_=clock_wide[h][:, block * P : (block + 1) * P], func=ACT.Abs,
-                                 scale=-1.0, bias=marks[:, 0, s : s + 1])
+            if s % 2 == 0:
+                distance[s] = sbuf("distance", 2, [P, 2, P], F32)
+            nc.scalar.activation(out=distance[s - s % 2][:, s % 2, :], in_=clock_wide[h][:, block * P : (block + 1) * P],
+                                 func=ACT.Abs, scale=-1.0, bias=marks[:, 0, s : s + 1])
 
-        def job_diag(s):
+        def job_diagonal_pair(s):
             h, block = divmod(s, BLOCKS)
-            nc.scalar.activation(out=diag[h][:, block * P : (block + 1) * P], in_=dist[s][:], func=ACT.Exp, scale=-1.0)
+            nc.scalar.activation(out=diagonal[h][:, block * P : (block + 2) * P], in_=distance[s][:].rearrange("p b j -> p (b j)"),
+                                 func=ACT.Exp, scale=-1.0)
 
-        def job_row(h, row, first, width, side, ref_block):
-            seg = slice(first, first + width)
-            n = h * BLOCKS + ref_block
+        def job_key_factor(h, side, block):
+            cols = slice(block * P, (block + 1) * P)
+            n = h * BLOCKS + block
             if side == START:
-                nc.scalar.activation(out=far_rows[h][:, row, seg], in_=clock_wide[h][:, seg], func=ACT.Exp,
-                                     scale=-1.0, bias=marks[:, 1, n : n + 1])
+                scale, bias = -1.0, marks[:, 1 + START, n : n + 1]
             else:
-                nc.scalar.activation(out=far_rows[h][:, row, seg], in_=clock_wide[h][:, seg], func=ACT.Exp,
-                                     scale=1.0, bias=neg_end[:, n : n + 1])
+                scale, bias = 1.0, neg_end[:, n : n + 1]
+            nc.scalar.activation(out=key_factor[h][:, side, cols], in_=clock_wide[h][:, cols], func=ACT.Exp, scale=scale, bias=bias)
 
-        jobs = [(0, P, job_open_head, (0,)), (0, P, job_dist, (0,))]
-        made = set()
+        jobs = [(0, P, job_open_head, (0,)), (0, P, job_distance, (0,)), (0, P, job_distance, (1,))]
         for s in range(STEPS):
             h, block = divmod(s, BLOCKS)
             if block == 0:
-                jobs.append((s, P, job_near, (h,)))
-            fresh = []
-            for seg in sorted(far_segments(block), key=lambda part: part[1]):
-                if (h, seg[0], seg[1]) not in made:
-                    made.add((h, seg[0], seg[1]))
-                    fresh.append((s, seg[2], job_row, (h,) + seg))
-            jobs.extend(fresh[:1])
-            jobs.append((s, P, job_diag, (s,)))
-            jobs.extend(fresh[1:])
-            if s + 1 < STEPS:
+                jobs.append((s, P, job_query_factor, (h,)))
+                rows = [(s, P, job_key_factor, (h, START, later)) for later in range(1, BLOCKS)]
+            else:
+                rows = [(s, P, job_key_factor, (h, END, block - 1))]
+            jobs.extend(rows[:1])
+            if s % 2 == 0:
+                jobs.append((s, 2 * P, job_diagonal_pair, (s,)))
+            jobs.extend(rows[1:])
+            if s % 2 == 1 and s + 1 < STEPS:
                 if block == BLOCKS - 1:
                     jobs.append((s, P, job_open_head, (h + 1,)))
-                jobs.append((s, P, job_dist, (s + 1,)))
-        per_step = sum(job[1] for job in jobs) // STEPS
-        done = [0, 0]
+                jobs.append((s, P, job_distance, (s + 1,)))
+                jobs.append((s, P, job_distance, (s + 2,)))
+        columns_per_step = sum(job[1] for job in jobs) // STEPS
+        progress = {"jobs": 0, "columns": 0}
 
-        def run_jobs(needed, target, head_limit):
-            while done[0] < len(jobs):
-                s, width, fn, args = jobs[done[0]]
-                if s > needed and (done[1] + width > target or s // BLOCKS > head_limit):
+        def run_jobs(due, budget):
+            while progress["jobs"] < len(jobs):
+                s, columns, function, arguments = jobs[progress["jobs"]]
+                if s > due and progress["columns"] + columns > budget:
                     break
-                fn(*args)
-                done[0] += 1
-                done[1] += width
+                function(*arguments)
+                progress["jobs"] += 1
+                progress["columns"] += columns
 
-        grouped_in, codes, scales = {}, {}, {}
+        turned_in, grouped_in, codes, scales = {}, {}, {}, {}
 
-        turned_in = {}
-
-        def turn_in(which, h, half, b, tag=None):
-            words = raw_in[which, h, half][:, b, :].bitcast(F32)
+        def turn_in(which, h, half, unit, tag=None):
+            pairs = raw_in[which, h, half][:, unit, :].bitcast(F32)
             if tag is None:
-                turned_in[which, h, half, b] = psum("turn_in", 2, [P, 4, P], F32)
+                bank = rotating_bank("turn_in", [P, 4, P], F32)
             else:
-                turned_in[which, h, half, b] = ps.tile([P, 4, P], F32, name="early_" + tag, tag=tag)
+                bank = named_bank(tag, "early_" + tag, [P, 4, P], F32)
+            turned_in[which, h, half, unit] = bank
             for j in range(2):
                 for u in range(2):
-                    nc.tensor.transpose(turned_in[which, h, half, b][:, 2 * j + u, :],
-                                        words[:, 256 * j + u : 256 * (j + 1) : 2], ident_f32[:])
+                    nc.tensor.transpose(bank[:, 2 * j + u, :], pairs[:, 256 * j + u : 256 * (j + 1) : 2], ident_f32[:])
 
-        def copy_in(which, h, half, b, engine_copy):
-            if b == 0:
+        def copy_in(which, h, half, unit, copy):
+            if unit == 0:
                 grouped_in[which, h, half] = sbuf("grouped_in", 4, [P, 4 * HALF], BF16)
-            words = grouped_in[which, h, half][:].bitcast(F32)
+            pairs = grouped_in[which, h, half][:].bitcast(F32)
             if (which, h, half) in by_units:
-                target = words.rearrange("k (b p a) -> k b p a", b=2, a=4)[:, b, :, :]
+                target = pairs.rearrange("k (b p a) -> k b p a", b=2, a=4)[:, unit, :, :]
             else:
-                target = words.rearrange("k (p b a) -> k b p a", b=2, a=4)[:, b, :, :]
-            engine_copy(out=target, in_=turned_in[which, h, half, b][:].rearrange("k a p -> k p a"))
+                target = pairs.rearrange("k (p b a) -> k b p a", b=2, a=4)[:, unit, :, :]
+            copy(out=target, in_=turned_in[which, h, half, unit][:].rearrange("k a p -> k p a"))
 
-        def quantize_in(which, h, half, first, count):
-            if first == 0:
+        def quantize_in(which, h, half, units=both):
+            if units.start == 0:
                 codes[which, h, half] = sbuf("codes_" + which, 4, [P, HALF], U32)
                 scales[which, h, half] = sbuf("scales_" + which, 4, [P, HALF], U8)
-            rows = slice(first * UNIT, (first + count) * UNIT)
+            rows = slice(units.start * UNIT, units.stop * UNIT)
             nc.vector.quantize_mx(out=codes[which, h, half][:, rows].bitcast(FP8X4), scales=scales[which, h, half][:, rows],
-                                  in_=grouped_in[which, h, half][:, 4 * first * UNIT : 4 * (first + count) * UNIT])
+                                  in_=grouped_in[which, h, half][:, 4 * rows.start : 4 * rows.stop])
 
-        raw = {}
+        scores, y, rounded = {}, {}, {}
 
         def multiply(s, g):
             h, block = divmod(s, BLOCKS)
             half, place = divmod(block, 4)
             cols = slice(place * P, (place + 1) * P)
-            raw[s, g] = ps.tile([P, HALF], F32, name="raw_%d_%d" % (s, g), tag="raw%d%d" % (s % 2, g))
-            nc.tensor.matmul_mx(out=raw[s, g][:], lhsT=codes["q", h, half][:, cols].bitcast(FP8X4), lhsT_scale=scales["q", h, half][:, cols],
+            scores[s, g] = named_bank("scores%d%d" % (s % 2, g), "scores_%d_%d" % (s, g), [P, HALF], F32)
+            nc.tensor.matmul_mx(out=scores[s, g][:],
+                                lhsT=codes["q", h, half][:, cols].bitcast(FP8X4), lhsT_scale=scales["q", h, half][:, cols],
                                 rhs=codes["k", h, g][:].bitcast(FP8X4), rhs_scale=scales["k", h, g][:], start=True, stop=True)
-
-        y, y_pair = {}, {}
 
         def weigh(s, g):
             h, block = divmod(s, BLOCKS)
             if g == 0:
-                if s % 2 == 0:
-                    y_pair[s] = sbuf("y", Y_BUFS // 2, [P, 2, T], F32)
-                y[s] = y_pair[s - s % 2][:, s % 2, :]
-            parts = far_segments(block) + [(None, block * P, P, None, None)]
-            for row, first, width, side, ref_block in sorted(parts, key=lambda part: part[1]):
-                if first // HALF != g:
-                    continue
-                seg = slice(first, first + width)
-                scores = raw[s, g][:, first % HALF : first % HALF + width]
-                if row is None:
-                    nc.vector.tensor_tensor(out=y[s][:, seg], in0=scores, in1=diag[h][:, seg], op=ALU.mult)
+                y[s] = sbuf("y", Y_SLOTS, [P, T], F32)
+            for place in range(4):
+                key_block = 4 * g + place
+                cols = slice(key_block * P, (key_block + 1) * P)
+                raw = scores[s, g][:, place * P : (place + 1) * P]
+                if key_block == block:
+                    nc.vector.tensor_tensor(out=y[s][:, cols], in0=raw, in1=diagonal[h][:, cols], op=ALU.mult)
                 else:
-                    n = (block * 2 + side) * BLOCKS + ref_block
-                    nc.vector.scalar_tensor_tensor(out=y[s][:, seg], in0=scores, scalar=near[:, h, n : n + 1],
-                                                   in1=far_rows[h][:, row, seg], op0=ALU.mult, op1=ALU.mult)
+                    side = START if key_block > block else END
+                    n = (block * 2 + side) * BLOCKS + key_block
+                    nc.vector.scalar_tensor_tensor(out=y[s][:, cols], in0=raw, scalar=query_factor[:, h, n : n + 1],
+                                                   in1=key_factor[h][:, side, cols], op0=ALU.mult, op1=ALU.mult)
 
         def store_y(s, cols):
             h, block = divmod(s, BLOCKS)
             nc.sync.dma_start(out=out_0[h, block * P : (block + 1) * P, cols], in_=y[s][:, cols])
 
-        rounded = {}
+        def gpsimd_round(out, in_):
+            nc.gpsimd.tensor_scalar(out=out, in0=in_, scalar1=1.0, scalar2=1.0, op0=ALU.mult, op1=ALU.mult)
 
-        def round_y(s, engine, first, last):
+        def round_y(s, first, last, copy):
             if s not in rounded:
                 rounded[s] = sbuf("rounded", 3, [P, T], BF16)
-            target = rounded[s][:].rearrange("i (u a e) -> i u a e", u=2, e=2)[:, :, first:last, :]
-            values = y[s][:].rearrange("i (a u e) -> i u a e", u=2, e=2)[:, :, first:last, :]
-            if engine == "gpsimd":
-                nc.gpsimd.tensor_scalar(out=target, in0=values, scalar1=1.0, scalar2=1.0, op0=ALU.mult, op1=ALU.mult)
-            elif engine == "vector":
-                vcopy(out=target, in_=values)
-            else:
-                scopy(out=target, in_=values)
+            copy(out=rounded[s][:].rearrange("i (u a e) -> i u a e", u=2, e=2)[:, :, first:last, :],
+                 in_=y[s][:].rearrange("i (a u e) -> i u a e", u=2, e=2)[:, :, first:last, :])
+
+        def scalar_words(s):
+            return WORDS - GPSIMD_WORDS_AT.get(s, GPSIMD_WORDS)
 
         group_of = {}
         for h in range(H):
@@ -296,167 +281,149 @@ def tile_bidirectional_decay_scores_g1_kernel(tc, queries, keys, clock, out_0, o
                 for s in range(first, first + size):
                     group_of[s] = (first, size)
                 first += size
-        grouped_out, out_words, out_scales = {}, {}, {}
+        turned_out, grouped_out, out_words, out_scales = {}, {}, {}, {}
 
-        turned_out = {}
-
-        def turn_out(s, halves, tag):
-            words = rounded[s][:].bitcast(F32)
-            turned_out[s, halves.start] = psum(tag, 2, [P, 2, 2, P], F32)
+        def turn_out(s, halves, family):
+            pairs = rounded[s][:].bitcast(F32)
+            bank = rotating_bank(family, [P, 2, 2, P], F32)
+            turned_out[s, halves.start] = bank
             for g in range(halves.start, halves.stop):
                 for u in range(2):
-                    at = 256 * u + P * g
-                    nc.tensor.transpose(turned_out[s, halves.start][:, g, u, :], words[:, at : at + P], ident_f32[:])
+                    at = WORDS * u + P * g
+                    nc.tensor.transpose(bank[:, g, u, :], pairs[:, at : at + P], ident_f32[:])
 
-        def copy_out(s, halves, engine_copy):
+        def copy_out(s, halves, copy):
             first, size = group_of[s]
             if first not in grouped_out:
                 grouped_out[first] = sbuf("grouped_out", 2, [P, 2, 4 * size * P], BF16)
             place = s - first
             target = grouped_out[first][:, halves, 4 * place * P : 4 * (place + 1) * P].bitcast(F32)
-            engine_copy(out=target.rearrange("k g (r u) -> k g r u", u=2),
-                        in_=turned_out[s, halves.start][:, halves, :, :].rearrange("k g u r -> k g r u"))
+            copy(out=target.rearrange("k g (r u) -> k g r u", u=2),
+                 in_=turned_out[s, halves.start][:, halves, :, :].rearrange("k g u r -> k g r u"))
 
-        words_hbm = out_1.rearrange("g p m t -> p g (m t)")
-
-        def store_words(halves, first, blocks, words):
-            nc.sync.dma_start(out=words_hbm[:, halves, 4 * first * P : 4 * (first + blocks) * P].bitcast(I32), in_=words.bitcast(I32))
-
-        def quantize_out(start, blocks, g, words):
-            first = group_of[start][0]
-            h, block = divmod(start, BLOCKS)
+        def quantize_out(first, g):
+            size = group_of[first][1]
+            h, block = divmod(first, BLOCKS)
             if h not in out_scales:
                 out_scales[h] = sbuf("out_scales", H, [P, 2, T], U8)
-            place = start - first
-            nc.vector.quantize_mx(out=words.bitcast(FP8X4), scales=out_scales[h][:, g, block * P : (block + blocks) * P],
-                                  in_=grouped_out[first][:, g, 4 * place * P : 4 * (place + blocks) * P])
+            if g == 0:
+                out_words[first] = sbuf("out_words", 3, [P, 2, size * P], U32)
+            nc.vector.quantize_mx(out=out_words[first][:, g, :].bitcast(FP8X4),
+                                  scales=out_scales[h][:, g, block * P : (block + size) * P], in_=grouped_out[first][:, g, :])
+
+        def store_words(first, halves):
+            size = group_of[first][1]
+            byte_cols = slice(4 * first * P, 4 * (first + size) * P)
+            nc.sync.dma_start(out=out_1.rearrange("g p m t -> p g (m t)")[:, halves, byte_cols].bitcast(I32),
+                              in_=out_words[first][:, halves, :].bitcast(I32))
 
         def store_scales(h):
             for r in range(4):
-                nc.sync.dma_start(
-                    out=out_2[:, r:16:4, h * T : (h + 1) * T].rearrange("g q m -> q g m").bitcast(I32),
-                    in_=out_scales[h][r:P:32, :, :].bitcast(I32))
+                nc.sync.dma_start(out=out_2[:, r:16:4, h * T : (h + 1) * T].rearrange("g q m -> q g m").bitcast(I32),
+                                  in_=out_scales[h][r:P:32, :, :].bitcast(I32))
 
-        def finish_half(first, g):
-            size = group_of[first][1]
-            if g == 0:
-                out_words[first] = sbuf("out_words", 3, [P, 2, size * P], U32)
-            quantize_out(first, size, g, out_words[first][:, g, :])
-            if g == 1:
-                store_words(slice(0, 2), first, size, out_words[first][:])
-                if (first + size) % BLOCKS == 0:
-                    store_scales(first // BLOCKS)
+        def finish_half_group(first, g):
+            quantize_out(first, g)
+            store_words(first, slice(g, g + 1))
+            if g == 1 and (first + group_of[first][1]) % BLOCKS == 0:
+                store_scales(first // BLOCKS)
 
-        both = slice(0, 2)
         turn_in("k", 0, 0, 0)
-        spread_clock(0, "raw10")
-        copy_in("k", 0, 0, 0, vcopy)
-        keep_clock(0, scopy)
+        spread_clock(0, "scores10")
+        copy_in("k", 0, 0, 0, vector_copy)
+        keep_clock(0, scalar_copy)
         turn_in("k", 0, 0, 1)
-        spread_clock(1, "raw00")
-        copy_in("k", 0, 0, 1, vcopy)
-        turn_in("q", 0, 0, 0, "raw01")
-        copy_in("q", 0, 0, 0, vcopy)
-        run_jobs(-1, 896, 0)
-        keep_clock(1, scopy)
-        quantize_in("k", 0, 0, 0, 2)
-        turn_in("k", 0, 1, 0, "raw11")
+        spread_clock(1, "scores00")
+        copy_in("k", 0, 0, 1, vector_copy)
+        turn_in("q", 0, 0, 0, "scores01")
+        copy_in("q", 0, 0, 0, vector_copy)
+        run_jobs(-1, 9 * P)
+        keep_clock(1, scalar_copy)
+        quantize_in("k", 0, 0)
+        turn_in("k", 0, 1, 0, "scores11")
         spread_clock(2, "turn_out0")
         spread_clock(3, "turn_out1")
-        copy_in("k", 0, 1, 0, scopy)
-        quantize_in("q", 0, 0, 0, 1)
+        copy_in("k", 0, 1, 0, scalar_copy)
+        quantize_in("q", 0, 0, slice(0, 1))
         turn_in("k", 0, 1, 1)
-        copy_in("k", 0, 1, 1, scopy)
-        keep_clock(2, vcopy)
+        copy_in("k", 0, 1, 1, scalar_copy)
+        keep_clock(2, vector_copy)
         multiply(0, 0)
         multiply(1, 0)
         turn_in("q", 0, 0, 1)
         turn_in("q", 0, 1, 0, "turn_out0")
-        run_jobs(1, 0, 0)
+        run_jobs(1, 0)
         weigh(0, 0)
-        quantize_in("k", 0, 1, 0, 2)
-        copy_in("q", 0, 0, 1, scopy)
+        quantize_in("k", 0, 1)
+        copy_in("q", 0, 0, 1, scalar_copy)
         multiply(0, 1)
         multiply(1, 1)
-        keep_clock(3, vcopy)
+        keep_clock(3, vector_copy)
         weigh(1, 0)
         turn_in("q", 0, 1, 1, "turn_out1")
-        quantize_in("q", 0, 0, 1, 1)
-        copy_in("q", 0, 1, 0, scopy)
-        copy_in("q", 0, 1, 1, scopy)
-        ahead = done[1]
+        quantize_in("q", 0, 0, slice(1, 2))
+        copy_in("q", 0, 1, 0, scalar_copy)
+        copy_in("q", 0, 1, 1, scalar_copy)
+        columns_at_start = progress["columns"]
 
-        units = []
-        for h in range(1, H):
-            for which, half in (("k", 0), ("k", 1), ("q", 0), ("q", 1)):
-                units.extend([(which, h, half, 0), (which, h, half, 1)])
-        on_vector = (1,5)
-        halves_in = [("q", 0, 1)] + [unit[0:3] for unit in units[0::2]]
-        quant_at = {}
-        for step, half in zip((2,3,4,6,8,10,12,14,16,18,20,22,24), halves_in):
-            quant_at[step] = (quantize_in, half + (0, 2))
-        outs = [(first, g) for first in (0,4,8,12,16,20,24,26) for g in range(2)]
-        for step, out in zip((7,9,11,13,15,17,19,21,23,25,26,27,28,29,30), outs):
-            quant_at[step] = (finish_half, out)
+        halves_in = [(which, h, half) for h in range(1, H) for which in ("k", "q") for half in range(2)]
+        units = [half + (unit,) for half in halves_in for unit in range(2)]
+        quantize_at = {}
+        for s, half in zip(QUANTIZE_IN_STEPS, [("q", 0, 1)] + halves_in):
+            quantize_at[s] = (quantize_in, half)
+        half_groups = [(first, g) for first in sorted(set(first for first, size in group_of.values())) for g in range(2)]
+        for s, half_group in zip(QUANTIZE_OUT_STEPS, half_groups):
+            quantize_at[s] = (finish_half_group, half_group)
+
+        last = STEPS - 1
         turn_in(*units[0])
-        shares = {0: 200, 1: 128, 5: 240,9:248,13:248,17:248,21:248}
-
-        def split(s):
-            return shares.get(s, 192)
-
-        for s in range(STEPS):
-            if s < len(units) and s not in on_vector:
-                copy_in(*units[s], scopy)
-            if 0 < s < STEPS - 1:
-                round_y(s - 1, "scalar", 0, 256 - split(s - 1))
+        for s in range(last):
+            if s < len(units) and s not in COPY_IN_ON_VECTOR:
+                copy_in(*units[s], scalar_copy)
+            if s >= 1:
+                round_y(s - 1, 0, scalar_words(s - 1), scalar_copy)
             if s >= 3:
-                copy_out(s - 3, both, vcopy if s in (10,14,18,22) else scopy)
-            if 0 < s < STEPS - 1:
+                copy_out(s - 3, both, vector_copy if s in COPY_OUT_ON_VECTOR else scalar_copy)
+            if s >= 1:
                 multiply(s + 1, 0)
                 multiply(s + 1, 1)
             if s >= 2:
                 turn_out(s - 2, both, "turn_out")
             if s + 1 < len(units):
                 turn_in(*units[s + 1])
-            run_jobs(s + 2, ahead + min(per_step + 0, per_step + 0 // (s + 1)) * (s + 1), H)
-            if s == STEPS - 1:
-                break
-            if s > 1:
+            run_jobs(s + 2, columns_at_start + columns_per_step * (s + 1))
+            if s >= 2:
                 weigh(s, 0)
             weigh(s, 1)
-            if s >= 20:
-                store_y(s, slice(0, T))
-            elif s % 2 == 1:
-                h, block = divmod(s - 1, BLOCKS)
-                nc.sync.dma_start(out=out_0[h, block * P : (block + 2) * P, :].rearrange("(b p) j -> p b j", b=2), in_=y_pair[s - 1][:])
-            round_y(s, "gpsimd", 256 - split(s), 256)
-            if s in on_vector:
-                copy_in(*units[s], vcopy)
-            if s in quant_at:
-                quant_at[s][0](*quant_at[s][1])
+            store_y(s, slice(0, T))
+            round_y(s, scalar_words(s), WORDS, gpsimd_round)
+            if s in COPY_IN_ON_VECTOR:
+                copy_in(*units[s], vector_copy)
+            if s in quantize_at:
+                function, arguments = quantize_at[s]
+                function(*arguments)
 
-        last = STEPS - 1
+        copy_out(last - 3, both, scalar_copy)
+        turn_out(last - 2, both, "turn_out")
         weigh(last, 0)
         store_y(last, slice(0, HALF))
-        round_y(last - 1, "scalar", 0, 256 - split(last - 1))
-        round_y(last, "scalar", 0, P)
-        copy_out(last - 2, both, scopy)
+        round_y(last - 1, 0, scalar_words(last - 1), scalar_copy)
+        round_y(last, 0, P, scalar_copy)
+        copy_out(last - 2, both, scalar_copy)
         weigh(last, 1)
         store_y(last, slice(HALF, T))
-        finish_half(last - 5, 1)
-        round_y(last, "vector", P, 256)
+        finish_half_group(last - 5, 1)
+        round_y(last, P, WORDS, vector_copy)
         turn_out(last - 1, both, "turn_out")
         turn_out(last, slice(0, 1), "turn_in")
         turn_out(last, slice(1, 2), "turn_in")
-        before = sbuf("out_words", 3, [P, 2, 2 * P], U32)
-        quantize_out(last - 3, 2, 0, before[:, 0, :])
-        quantize_out(last - 3, 2, 1, before[:, 1, :])
-        store_words(both, last - 3, 2, before[:])
-        copy_out(last - 1, both, scopy)
-        copy_out(last, slice(0, 1), vcopy)
-        copy_out(last, slice(1, 2), scopy)
-        final = sbuf("out_words", 3, [P, 2, 2 * P], U32)
-        quantize_out(last - 1, 2, 0, final[:, 0, :])
-        quantize_out(last - 1, 2, 1, final[:, 1, :])
-        store_words(both, last - 1, 2, final[:])
+        quantize_out(last - 3, 0)
+        quantize_out(last - 3, 1)
+        store_words(last - 3, both)
+        copy_out(last - 1, both, scalar_copy)
+        copy_out(last, slice(0, 1), vector_copy)
+        copy_out(last, slice(1, 2), scalar_copy)
+        quantize_out(last - 1, 0)
+        quantize_out(last - 1, 1)
+        store_words(last - 1, both)
         store_scales(H - 1)

@@ -31,7 +31,6 @@ COPY_IN_ON_VECTOR = (1, 5)
 COPY_OUT_ON_VECTOR = (12, 20)
 QUANTIZE_IN_STEPS = (2, 3) + tuple(range(4, 25, 2))
 QUANTIZE_OUT_STEPS = tuple(range(7, 26, 2)) + (26, 27, 28, 29, 30)
-WARM_PASSES = 8
 
 
 def tile_bidirectional_decay_scores_g1_kernel(tc, queries, keys, clock, out_0, out_1, out_2):
@@ -86,24 +85,13 @@ def tile_bidirectional_decay_scores_g1_kernel(tc, queries, keys, clock, out_0, o
                 for half in range(2):
                     raw_in[which, h, half] = whole[:, half, :, :]
 
-        ones = sbuf("ones", 1, [P, 4 * P], BF16)
-        nc.vector.memset(ones[:].bitcast(F32), 1.0)
-        table_warm = sbuf("table_warm", 1, [P, 1], F32)
-        nc.scalar.activation(out=table_warm[:], in_=ones[:, 0:1], func=ACT.Exp)
         ident_bf = sbuf("ident_bf", 1, [P, P], BF16)
         ident_f32 = sbuf("ident_f32", 1, [P, P], F32)
         make_identity(nc, ident_bf[:])
         make_identity(nc, ident_f32[:])
-        warm_codes = sbuf("warm_codes", 1, [P, P], U32)
-        warm_scales = sbuf("warm_scales", 1, [P, P], U8)
-        nc.vector.quantize_mx(out=warm_codes[:].bitcast(FP8X4), scales=warm_scales[:], in_=ones[:])
         for tile in (clock_rows, clock_pairs):
             nc.vector.memset(tile[32:64, :], 0.0)
             nc.vector.memset(tile[64:P, :], 0.0)
-        warm_bank = named_bank("scores00", "warm_bank", [P, 4, P], F32)
-        for n in range(WARM_PASSES):
-            nc.tensor.matmul_mx(out=warm_bank[:, n % 4, :], lhsT=warm_codes[:].bitcast(FP8X4), lhsT_scale=warm_scales[:],
-                                rhs=warm_codes[:].bitcast(FP8X4), rhs_scale=warm_scales[:], start=True, stop=True)
 
         marks_bank = rotating_bank("turn_out", [P, 3, P], BF16)
         nc.tensor.transpose(marks_bank[:, 0, :], clock_rows[:], ident_bf[:])
@@ -331,6 +319,7 @@ def tile_bidirectional_decay_scores_g1_kernel(tc, queries, keys, clock, out_0, o
         turn_in("k", 0, 0, 0)
         spread_clock(0, "scores10")
         copy_in("k", 0, 0, 0, vector_copy)
+        run_jobs(-1, P)
         keep_clock(0, scalar_copy)
         turn_in("k", 0, 0, 1)
         spread_clock(1, "scores00")

from contextlib import ExitStack

import concourse.mybir as mybir
from concourse.masks import make_identity

H, T, DK = 4, 1024, 512
FLOPS = 2 * H * T * T * DK

F32 = mybir.dt.float32
BF16 = mybir.dt.bfloat16
I32 = mybir.dt.int32
U32 = mybir.dt.uint32
U8 = mybir.dt.uint8
FP8X4 = mybir.dt.float8_e4m3fn_x4
ALU = mybir.AluOpType
ACT = mybir.ActivationFunctionType

P = 128
BLOCKS = T // P
STEPS = H * BLOCKS
HALF = 512
UNIT = 256
WORDS = T // 4
START, END = 0, 1

Y_SLOTS = 10
GROUPS = [[4, 4], [4, 4], [4, 4], [2, 2, 2, 2]]
GPSIMD_WORDS = 208
GPSIMD_WORDS_AT = {0: 200, 1: 128, 5: 240, 11: 248, 19: 248}
COPY_IN_ON_VECTOR = (1, 5)
COPY_OUT_ON_VECTOR = (12, 20)
QUANTIZE_IN_STEPS = (2, 3) + tuple(range(4, 25, 2))
QUANTIZE_OUT_STEPS = tuple(range(7, 26, 2)) + (26, 27, 28, 29, 30)


def tile_bidirectional_decay_scores_g1_kernel(tc, queries, keys, clock, out_0, out_1, out_2):
    nc = tc.nc
    with ExitStack() as ctx:
        sb = ctx.enter_context(tc.tile_pool(name="sb", bufs=1))
        ps = ctx.enter_context(tc.psum_pool(name="ps", bufs=1))
        ctx.enter_context(tc.manual_schedule())

        taken = {}

        def next_slot(family, slots):
            n = taken.get(family, 0)
            taken[family] = n + 1
            return dict(name="%s_%d" % (family, n), tag="%s%d" % (family, n % slots))

        def sbuf(family, slots, shape, dtype):
            return sb.tile(shape, dtype, align_bytes=64, **next_slot(family, slots))

        def rotating_bank(family, shape, dtype):
            return ps.tile(shape, dtype, **next_slot(family, 2))

        def named_bank(tag, name, shape, dtype):
            return ps.tile(shape, dtype, name=name, tag=tag)

        vector_copy, scalar_copy = nc.vector.tensor_copy, nc.scalar.copy
        both = slice(0, 2)

        source = {"q": queries, "k": keys}
        raw_in = {}
        by_units = [("k", 0, 0), ("q", 0, 0), ("k", 0, 1)]

        clock_rows = sbuf("clock_rows", 1, [P, P], BF16)
        nc.sync.dma_start(out=clock_rows[0:STEPS, :], in_=clock.rearrange("h (b p) -> (h b) p", p=P))
        clock_pairs = sbuf("clock_pairs", 1, [P, 2 * P], BF16)
        for part in range(2):
            nc.scalar.dma_start(out=clock_pairs[16 * part : 16 * part + 16, :], in_=clock.rearrange("h (b p) -> (h b) p", p=2 * P))
        for which, h, half, unit in (("k", 0, 0, 0), ("k", 0, 0, 1), ("q", 0, 0, 0), ("k", 0, 1, 0), ("k", 0, 1, 1), ("q", 0, 0, 1)):
            if unit == 0:
                raw_in[which, h, half] = sbuf("raw_half", 4, [P, 2, 2 * DK], BF16)
            first = half * HALF + unit * UNIT
            nc.sync.dma_start(out=raw_in[which, h, half][:, unit, :],
                              in_=source[which][h, first : first + UNIT, :].rearrange("(p j) c -> p (j c)", j=2))
        raw_in["q", 0, 1] = sbuf("raw_half", 4, [P, 2, 2 * DK], BF16)
        nc.sync.dma_start(out=raw_in["q", 0, 1][:].rearrange("p b x -> p (b x)"),
                          in_=queries[0, HALF:T, :].rearrange("(p j) c -> p (j c)", j=4))
        for h in range(1, H):
            for which in ("k", "q"):
                whole = sbuf("raw_head", 2 * (H - 1), [P, 2, 2, 2 * DK], BF16)
                nc.sync.dma_start(out=whole[:].rearrange("p a b x -> p a (b x)"),
                                  in_=source[which][h, :, :].rearrange("(a p j) c -> p a (j c)", a=2, j=4))
                for half in range(2):
                    raw_in[which, h, half] = whole[:, half, :, :]

        ident_bf = sbuf("ident_bf", 1, [P, P], BF16)
        ident_f32 = sbuf("ident_f32", 1, [P, P], F32)
        make_identity(nc, ident_bf[:])
        make_identity(nc, ident_f32[:])
        for tile in (clock_rows, clock_pairs):
            nc.vector.memset(tile[32:64, :], 0.0)
            nc.vector.memset(tile[64:P, :], 0.0)

        marks_bank = rotating_bank("turn_out", [P, 3, P], BF16)
        nc.tensor.transpose(marks_bank[:, 0, :], clock_rows[:], ident_bf[:])
        nc.tensor.transpose(marks_bank[:, 1 + START, :], clock_rows[:, 0:1].to_broadcast([P, P]), ident_bf[:])
        nc.tensor.transpose(marks_bank[:, 1 + END, :], clock_rows[:, P - 1 : P].to_broadcast([P, P]), ident_bf[:])
        pair_bank = rotating_bank("turn_out", [P, P], F32)
        nc.tensor.transpose(pair_bank[:], clock_pairs[:].bitcast(F32), ident_f32[:])
        pair_cols = sbuf("pair_cols", 1, [P, STEPS // 2], F32)
        vector_copy(out=pair_cols[:], in_=pair_bank[:, 0 : STEPS // 2])
        marks = sbuf("marks", 1, [P, 3, STEPS], BF16)
        vector_copy(out=marks[:], in_=marks_bank[:, :, 0:STEPS])
        neg_end = sbuf("neg_end", 1, [P, STEPS], F32)
        nc.gpsimd.tensor_scalar(out=neg_end[:], in0=marks[:, 1 + END, :], scalar1=-1.0, scalar2=1.0, op0=ALU.mult, op1=ALU.mult)
        gaps = sbuf("gaps", 1, [P, H, BLOCKS, 2, BLOCKS], F32)
        for h in range(H):
            blocks = slice(h * BLOCKS, (h + 1) * BLOCKS)
            nc.gpsimd.tensor_tensor(
                out=gaps[:, h, :, :, :],
                in0=marks[:, 0, blocks].unsqueeze(2).unsqueeze(3).to_broadcast([P, BLOCKS, 2, BLOCKS]),
                in1=marks[:, 1:3, blocks].unsqueeze(1).to_broadcast([P, BLOCKS, 2, BLOCKS]),
                op=ALU.subtract)

        clock_wide, wide_bank = {}, {}

        def spread_clock(h, tag):
            wide_bank[h] = named_bank(tag, "wide_%d" % h, [P, 4, P], F32)
            for b in range(4):
                column = pair_cols[:, 4 * h + b : 4 * h + b + 1]
                nc.tensor.transpose(wide_bank[h][:, b, :], column.to_broadcast([P, P]), ident_f32[:])

        def keep_clock(h, copy):
            clock_wide[h] = sbuf("clock_wide", H, [P, T], BF16)
            copy(out=clock_wide[h][:].bitcast(F32), in_=wide_bank[h][:].rearrange("p b x -> p (b x)"))

        query_factor = sbuf("query_factor", 1, [P, H, BLOCKS * 2 * BLOCKS], F32)
        key_factor, diagonal, distance, abs_gaps = {}, {}, {}, {}

        def job_open_head(h):
            key_factor[h] = sbuf("key_factor", 2, [P, 2, T], F32)
            diagonal[h] = sbuf("diagonal", 2, [P, T], F32)
            abs_gaps[h] = sbuf("abs_gaps", 2, [P, BLOCKS * 2 * BLOCKS], F32)
            nc.scalar.activation(out=abs_gaps[h][:], in_=gaps[:, h, :, :, :].rearrange("p i e j -> p (i e j)"), func=ACT.Abs)

        def job_query_factor(h):
            nc.scalar.activation(out=query_factor[:, h, :], in_=abs_gaps[h][:], func=ACT.Exp, scale=-1.0)

        def job_distance(s):
            h, block = divmod(s, BLOCKS)
            if s % 2 == 0:
                distance[s] = sbuf("distance", 2, [P, 2, P], F32)
            nc.scalar.activation(out=distance[s - s % 2][:, s % 2, :], in_=clock_wide[h][:, block * P : (block + 1) * P],
                                 func=ACT.Abs, scale=-1.0, bias=marks[:, 0, s : s + 1])

        def job_diagonal_pair(s):
            h, block = divmod(s, BLOCKS)
            nc.scalar.activation(out=diagonal[h][:, block * P : (block + 2) * P], in_=distance[s][:].rearrange("p b j -> p (b j)"),
                                 func=ACT.Exp, scale=-1.0)

        def job_key_factor(h, side, block):
            cols = slice(block * P, (block + 1) * P)
            n = h * BLOCKS + block
            if side == START:
                scale, bias = -1.0, marks[:, 1 + START, n : n + 1]
            else:
                scale, bias = 1.0, neg_end[:, n : n + 1]
            nc.scalar.activation(out=key_factor[h][:, side, cols], in_=clock_wide[h][:, cols], func=ACT.Exp, scale=scale, bias=bias)

        jobs = [(0, P, job_open_head, (0,)), (0, P, job_distance, (0,)), (0, P, job_distance, (1,))]
        for s in range(STEPS):
            h, block = divmod(s, BLOCKS)
            if block == 0:
                jobs.append((s, P, job_query_factor, (h,)))
                rows = [(s, P, job_key_factor, (h, START, later)) for later in range(1, BLOCKS)]
            else:
                rows = [(s, P, job_key_factor, (h, END, block - 1))]
            jobs.extend(rows[:1])
            if s % 2 == 0:
                jobs.append((s, 2 * P, job_diagonal_pair, (s,)))
            jobs.extend(rows[1:])
            if s % 2 == 1 and s + 1 < STEPS:
                if block == BLOCKS - 1:
                    jobs.append((s, P, job_open_head, (h + 1,)))
                jobs.append((s, P, job_distance, (s + 1,)))
                jobs.append((s, P, job_distance, (s + 2,)))
        columns_per_step = sum(job[1] for job in jobs) // STEPS
        progress = {"jobs": 0, "columns": 0}

        def run_jobs(due, budget):
            while progress["jobs"] < len(jobs):
                s, columns, function, arguments = jobs[progress["jobs"]]
                if s > due and progress["columns"] + columns > budget:
                    break
                function(*arguments)
                progress["jobs"] += 1
                progress["columns"] += columns

        turned_in, grouped_in, codes, scales = {}, {}, {}, {}

        def turn_in(which, h, half, unit, tag=None):
            pairs = raw_in[which, h, half][:, unit, :].bitcast(F32)
            if tag is None:
                bank = rotating_bank("turn_in", [P, 4, P], F32)
            else:
                bank = named_bank(tag, "early_" + tag, [P, 4, P], F32)
            turned_in[which, h, half, unit] = bank
            for j in range(2):
                for u in range(2):
                    nc.tensor.transpose(bank[:, 2 * j + u, :], pairs[:, 256 * j + u : 256 * (j + 1) : 2], ident_f32[:])

        def copy_in(which, h, half, unit, copy):
            if unit == 0:
                grouped_in[which, h, half] = sbuf("grouped_in", 4, [P, 4 * HALF], BF16)
            pairs = grouped_in[which, h, half][:].bitcast(F32)
            if (which, h, half) in by_units:
                target = pairs.rearrange("k (b p a) -> k b p a", b=2, a=4)[:, unit, :, :]
            else:
                target = pairs.rearrange("k (p b a) -> k b p a", b=2, a=4)[:, unit, :, :]
            copy(out=target, in_=turned_in[which, h, half, unit][:].rearrange("k a p -> k p a"))

        def quantize_in(which, h, half, units=both):
            if units.start == 0:
                codes[which, h, half] = sbuf("codes_" + which, 4, [P, HALF], U32)
                scales[which, h, half] = sbuf("scales_" + which, 4, [P, HALF], U8)
            rows = slice(units.start * UNIT, units.stop * UNIT)
            nc.vector.quantize_mx(out=codes[which, h, half][:, rows].bitcast(FP8X4), scales=scales[which, h, half][:, rows],
                                  in_=grouped_in[which, h, half][:, 4 * rows.start : 4 * rows.stop])

        scores, y, rounded = {}, {}, {}

        def multiply(s, g):
            h, block = divmod(s, BLOCKS)
            half, place = divmod(block, 4)
            cols = slice(place * P, (place + 1) * P)
            scores[s, g] = named_bank("scores%d%d" % (s % 2, g), "scores_%d_%d" % (s, g), [P, HALF], F32)
            nc.tensor.matmul_mx(out=scores[s, g][:],
                                lhsT=codes["q", h, half][:, cols].bitcast(FP8X4), lhsT_scale=scales["q", h, half][:, cols],
                                rhs=codes["k", h, g][:].bitcast(FP8X4), rhs_scale=scales["k", h, g][:], start=True, stop=True)

        def weigh(s, g):
            h, block = divmod(s, BLOCKS)
            if g == 0:
                y[s] = sbuf("y", Y_SLOTS, [P, T], F32)
            for place in range(4):
                key_block = 4 * g + place
                cols = slice(key_block * P, (key_block + 1) * P)
                raw = scores[s, g][:, place * P : (place + 1) * P]
                if key_block == block:
                    nc.vector.tensor_tensor(out=y[s][:, cols], in0=raw, in1=diagonal[h][:, cols], op=ALU.mult)
                else:
                    side = START if key_block > block else END
                    n = (block * 2 + side) * BLOCKS + key_block
                    nc.vector.scalar_tensor_tensor(out=y[s][:, cols], in0=raw, scalar=query_factor[:, h, n : n + 1],
                                                   in1=key_factor[h][:, side, cols], op0=ALU.mult, op1=ALU.mult)

        def store_y(s, cols):
            h, block = divmod(s, BLOCKS)
            nc.sync.dma_start(out=out_0[h, block * P : (block + 1) * P, cols], in_=y[s][:, cols])

        def gpsimd_round(out, in_):
            nc.gpsimd.tensor_scalar(out=out, in0=in_, scalar1=1.0, scalar2=1.0, op0=ALU.mult, op1=ALU.mult)

        def round_y(s, first, last, copy):
            if s not in rounded:
                rounded[s] = sbuf("rounded", 3, [P, T], BF16)
            copy(out=rounded[s][:].rearrange("i (u a e) -> i u a e", u=2, e=2)[:, :, first:last, :],
                 in_=y[s][:].rearrange("i (a u e) -> i u a e", u=2, e=2)[:, :, first:last, :])

        def scalar_words(s):
            return WORDS - GPSIMD_WORDS_AT.get(s, GPSIMD_WORDS)

        group_of = {}
        for h in range(H):
            first = h * BLOCKS
            for size in GROUPS[h]:
                for s in range(first, first + size):
                    group_of[s] = (first, size)
                first += size
        turned_out, grouped_out, out_words, out_scales = {}, {}, {}, {}

        def turn_out(s, halves, family):
            pairs = rounded[s][:].bitcast(F32)
            bank = rotating_bank(family, [P, 2, 2, P], F32)
            turned_out[s, halves.start] = bank
            for g in range(halves.start, halves.stop):
                for u in range(2):
                    at = WORDS * u + P * g
                    nc.tensor.transpose(bank[:, g, u, :], pairs[:, at : at + P], ident_f32[:])

        def copy_out(s, halves, copy):
            first, size = group_of[s]
            if first not in grouped_out:
                grouped_out[first] = sbuf("grouped_out", 2, [P, 2, 4 * size * P], BF16)
            place = s - first
            target = grouped_out[first][:, halves, 4 * place * P : 4 * (place + 1) * P].bitcast(F32)
            copy(out=target.rearrange("k g (r u) -> k g r u", u=2),
                 in_=turned_out[s, halves.start][:, halves, :, :].rearrange("k g u r -> k g r u"))

        def quantize_out(first, g):
            size = group_of[first][1]
            h, block = divmod(first, BLOCKS)
            if h not in out_scales:
                out_scales[h] = sbuf("out_scales", H, [P, 2, T], U8)
            if g == 0:
                out_words[first] = sbuf("out_words", 3, [P, 2, size * P], U32)
            nc.vector.quantize_mx(out=out_words[first][:, g, :].bitcast(FP8X4),
                                  scales=out_scales[h][:, g, block * P : (block + size) * P], in_=grouped_out[first][:, g, :])

        def store_words(first, halves):
            size = group_of[first][1]
            byte_cols = slice(4 * first * P, 4 * (first + size) * P)
            nc.sync.dma_start(out=out_1.rearrange("g p m t -> p g (m t)")[:, halves, byte_cols].bitcast(I32),
                              in_=out_words[first][:, halves, :].bitcast(I32))

        def store_scales(h):
            for r in range(4):
                nc.sync.dma_start(out=out_2[:, r:16:4, h * T : (h + 1) * T].rearrange("g q m -> q g m").bitcast(I32),
                                  in_=out_scales[h][r:P:32, :, :].bitcast(I32))

        def finish_half_group(first, g):
            quantize_out(first, g)
            store_words(first, slice(g, g + 1))
            if g == 1 and (first + group_of[first][1]) % BLOCKS == 0:
                store_scales(first // BLOCKS)

        turn_in("k", 0, 0, 0)
        spread_clock(0, "scores10")
        copy_in("k", 0, 0, 0, vector_copy)
        run_jobs(-1, P)
        keep_clock(0, scalar_copy)
        turn_in("k", 0, 0, 1)
        spread_clock(1, "scores00")
        copy_in("k", 0, 0, 1, vector_copy)
        turn_in("q", 0, 0, 0, "scores01")
        copy_in("q", 0, 0, 0, vector_copy)
        run_jobs(-1, 9 * P)
        keep_clock(1, scalar_copy)
        quantize_in("k", 0, 0)
        turn_in("k", 0, 1, 0, "scores11")
        spread_clock(2, "turn_out0")
        spread_clock(3, "turn_out1")
        copy_in("k", 0, 1, 0, scalar_copy)
        quantize_in("q", 0, 0, slice(0, 1))
        turn_in("k", 0, 1, 1)
        copy_in("k", 0, 1, 1, scalar_copy)
        keep_clock(2, vector_copy)
        multiply(0, 0)
        multiply(1, 0)
        turn_in("q", 0, 0, 1)
        turn_in("q", 0, 1, 0, "turn_out0")
        run_jobs(1, 0)
        weigh(0, 0)
        quantize_in("k", 0, 1)
        copy_in("q", 0, 0, 1, scalar_copy)
        multiply(0, 1)
        multiply(1, 1)
        keep_clock(3, vector_copy)
        weigh(1, 0)
        turn_in("q", 0, 1, 1, "turn_out1")
        quantize_in("q", 0, 0, slice(1, 2))
        copy_in("q", 0, 1, 0, scalar_copy)
        copy_in("q", 0, 1, 1, scalar_copy)
        columns_at_start = progress["columns"]

        halves_in = [(which, h, half) for h in range(1, H) for which in ("k", "q") for half in range(2)]
        units = [half + (unit,) for half in halves_in for unit in range(2)]
        quantize_at = {}
        for s, half in zip(QUANTIZE_IN_STEPS, [("q", 0, 1)] + halves_in):
            quantize_at[s] = (quantize_in, half)
        half_groups = [(first, g) for first in sorted(set(first for first, size in group_of.values())) for g in range(2)]
        for s, half_group in zip(QUANTIZE_OUT_STEPS, half_groups):
            quantize_at[s] = (finish_half_group, half_group)

        last = STEPS - 1
        turn_in(*units[0])
        for s in range(last):
            if s < len(units) and s not in COPY_IN_ON_VECTOR:
                copy_in(*units[s], scalar_copy)
            if s >= 1:
                round_y(s - 1, 0, scalar_words(s - 1), scalar_copy)
            if s >= 3:
                copy_out(s - 3, both, vector_copy if s in COPY_OUT_ON_VECTOR else scalar_copy)
            if s >= 1:
                multiply(s + 1, 0)
                multiply(s + 1, 1)
            if s >= 2:
                turn_out(s - 2, both, "turn_out")
            if s + 1 < len(units):
                turn_in(*units[s + 1])
            run_jobs(s + 2, columns_at_start + columns_per_step * (s + 1))
            if s >= 2:
                weigh(s, 0)
            weigh(s, 1)
            store_y(s, slice(0, T))
            round_y(s, scalar_words(s), WORDS, gpsimd_round)
            if s in COPY_IN_ON_VECTOR:
                copy_in(*units[s], vector_copy)
            if s in quantize_at:
                function, arguments = quantize_at[s]
                function(*arguments)

        copy_out(last - 3, both, scalar_copy)
        turn_out(last - 2, both, "turn_out")
        weigh(last, 0)
        store_y(last, slice(0, HALF))
        round_y(last - 1, 0, scalar_words(last - 1), scalar_copy)
        round_y(last, 0, P, scalar_copy)
        copy_out(last - 2, both, scalar_copy)
        weigh(last, 1)
        store_y(last, slice(HALF, T))
        finish_half_group(last - 5, 1)
        round_y(last, P, WORDS, vector_copy)
        turn_out(last - 1, both, "turn_out")
        turn_out(last, slice(0, 1), "turn_in")
        turn_out(last, slice(1, 2), "turn_in")
        quantize_out(last - 3, 0)
        quantize_out(last - 3, 1)
        store_words(last - 3, both)
        copy_out(last - 1, both, scalar_copy)
        copy_out(last, slice(0, 1), vector_copy)
        copy_out(last, slice(1, 2), scalar_copy)
        quantize_out(last - 1, 0)
        quantize_out(last - 1, 1)
        store_words(last - 1, both)
        store_scales(H - 1)
